import numpy as np, ml_dtypes
CORES = [66,74,82,90,194,202,210,218]
N = 8
import mx_ref
BF = ml_dtypes.bfloat16
def gentries(a):
    return np.ascontiguousarray(a.reshape(8, 16, -1).transpose(0, 2, 1)).reshape(8, -1)
def gtable(e):
    e = np.asarray(e); return np.ascontiguousarray(e.reshape(8, -1, 16).transpose(0, 2, 1)).reshape(128, -1).astype(np.int32)
def gcols(t, e):
    v = np.concatenate([t.reshape(8, 16, -1, 4), np.zeros((8, 16, 1, 4), BF)], axis=2)
    return np.ascontiguousarray(np.stack([v[g][:, e[g]] for g in range(8)])).reshape(128, -1)
def tile(rs):
    return np.stack(rs, axis=2).reshape(128, -1).astype(BF)
def pick(q, e):
    c = np.concatenate([q[0].reshape(128, -1, 4), np.zeros((128, 1, 4), np.uint8)], axis=1); s = np.concatenate([q[1], np.ones((16, 1), np.uint8)], axis=1)
    return (np.ascontiguousarray(c[:, e].reshape(128, -1)), np.ascontiguousarray(s[:, e]))
def join(*qs):
    return (np.concatenate([q[0] for q in qs], axis=1), np.concatenate([q[1] for q in qs], axis=1))
def put(q, e, v):
    c, s = q[0].reshape(128, -1, 4).copy(), q[1].copy(); c[:, e] = v[0].reshape(128, -1, 4); s[:, e] = v[1]
    return (c.reshape(128, -1), s)
def pk(c, s):
    return (np.ascontiguousarray(c), mx_ref.live(s))
def emit(q):
    return q[0], q[1]
def packed(v, rng):
    q = [mx_ref.quantize(np.ascontiguousarray(v[r])) for r in range(N)]
    return np.stack([a for a, b in q]), np.stack([mx_ref.plane(b, rng) for a, b in q])
def values_of_codes():
    e, c = np.zeros((128, 128, 4), np.float32), np.zeros((128, 2, 4), np.uint8)
    e[np.arange(128), np.arange(128), 0] = 1
    c[:127, :, 0] = np.arange(256).reshape(2, 128).T[:127]
    return mx_ref.matmul(mx_ref.quantize(e.reshape(128, 512).astype(BF)), (c.reshape(128, 8), np.full((16, 2), 127, np.uint8))).T.reshape(-1).astype(np.float64)
CODE_VALUE, SCALE_VALUE = values_of_codes(), 2.0 ** (np.arange(256) - 127.0)
def decode(q):
    return (CODE_VALUE[q[0]].reshape(16, 8, -1, 4) * SCALE_VALUE[q[1]][:, None, :, None] + 0.0).reshape(128, -1).astype(np.float32)
def f(rng, *shape):
    return mx_ref.flush((rng.standard_normal(shape, dtype=np.float32) * np.exp2(rng.integers(-2, 3, shape[:-1] + (1,)))).astype(BF))
def wide(rng, *shape, cols=0):
    v = rng.standard_normal(shape, dtype=np.float32) * np.exp2(rng.integers(-12, 13, shape)).astype(np.float32)
    if cols: v *= np.repeat(np.exp2(rng.integers(-cols, cols + 1, shape[:-2] + (1, shape[-1] // 4))) * (rng.random(shape[:-2] + (1, shape[-1] // 4)) > 0.0625), 4, axis=-1).astype(np.float32)
    return mx_ref.flush(v.astype(BF))
C, K, A, B, R = 224, 64, 4, 4, 3
STEP = [1, 2, 4]
def classes(key):
    c, one, two = np.zeros((8, C), int), np.full((8, K), -1), np.full((8, K), -1)
    for g in range(8):
        first, mine = np.unique(key[g], return_index=True, return_inverse=True)[1:]
        low = np.sort(first)
        c[g] = np.searchsorted(low, first[mine])
        for k in range(len(low)):
            m = np.flatnonzero(c[g] == k)
            one[g, k] = m[0]
            two[g, k] = m[min(1, len(m) - 1)]
    return c, one, two
def numbers_of(rng):
    return {"x": np.array(f(rng, N, 128, 4 * C)), "u": np.array(f(rng, N, 128, 512)), "v": np.array(f(rng, N, 128, 512))}
def lists_of(rng):
    return {"nx": rng.integers(0, C, (N, 8, C)), "co": rng.integers(0, K, (N, 8, C))}
def stored(l):
    return {k: np.stack([gtable(e) for e in l[k]]) for k in ("nx", "co")}
def weights(rng, w):
    c, p = packed(w, rng)
    return {"wc": c, "ws": p}
def quiet(rng):
    w = np.array(f(rng, N, 128, 2048)).reshape(N, 8, 16, 4, 8, 16, 4)
    w[:, :, :8] = 0
    w[:, :, :, :, :, :8] = 0
    return weights(rng, w.reshape(N, 128, 2048))
def marked(d, m, k):
    x = d["x"].reshape(N, 8, 16, C, 4)
    u = d["u"].reshape(N, 128, 128, 4)
    x[:, :, :8] = 0
    k = k.astype(np.float32)
    for i in range(2):
        x[:, :, i, :, :2] = m[:, :, :, i].astype(np.float32).astype(BF)
        u[:, :, i::16] = 0
        for h in range(i, 128, 16):
            u[:, h, h, 0] = k.astype(BF)
            u[:, h, h, 1] = (-k).astype(BF)
    return {"x": x.reshape(N, 128, 4 * C), "u": u.reshape(N, 128, 512), "v": d["v"]}
def setup_inputs(rng):
    return {**numbers_of(rng), **stored(lists_of(rng)), **weights(rng, f(rng, N, 128, 2048))}
def setup_inputs_full(rng):
    d, l = numbers_of(rng), lists_of(rng)
    o = rng.permutation(N)
    bits = np.zeros((N, 8, C), int)
    for r in range(N):
        e = np.argsort(rng.random((8, C)), axis=1)
        if o[r] % 4 == 3:
            l["co"][r] = rng.integers(0, K, (8, 1))
            bits[r] = e % (1 + rng.permutation(8) % 4)[:, None]
        else:
            k, one, two = classes(np.minimum(e, K - 1) if o[r] % 4 == 1 else e % K)
            l["co"][r] = k % A + A * rng.integers(0, K // A, (8, C))
            l["nx"][r] = np.take_along_axis(one, k // A % B + B * rng.integers(0, K // B, (8, C)), axis=1)
            bits[r] = k // (A * B)
    m = np.zeros((N, 8, C, 2, 2))
    m[:, :, :, 0] = 2 * (np.arange(2) == (bits >> 1)[:, :, :, None])
    m[:, :, :, 1] = 2 * (np.arange(2) == (bits & 1)[:, :, :, None])
    return {**marked(d, m, np.ones(N)), **stored(l), **quiet(rng)}
def setup_inputs_near(rng):
    d, l = numbers_of(rng), lists_of(rng)
    p = np.array([[0, 0], [2, 2], [3, 2], [2, 3], [2, 0], [0, 2]])
    e = np.argsort(rng.random((N, 8, C)), axis=2)
    h = np.argsort(rng.random((N, 8, C)), axis=2)
    m = np.stack([p[e // 4 % 6], p[h % 6]], axis=3) * 2.0 ** np.array([-30, -12, 0, 28])[e % 4][:, :, :, None, None]
    k = np.where(rng.permutation(N) < N // 2, 2.0 ** -30, 1.0)
    return {**marked(d, m, k), **stored(l), **quiet(rng)}
def setup_inputs_lists(rng):
    d, l = numbers_of(rng), lists_of(rng)
    o = rng.permutation(N)
    x = d["x"].reshape(N, 128, C, 4)
    for r in range(N):
        a = x[r][:, :2].copy()
        if o[r] % 4 == 0: l["nx"][r] = np.arange(C)
        if o[r] % 4 == 1: l["nx"][r] = rng.integers(0, C, (8, 1))
        if o[r] % 4 == 2:
            l["nx"][r] = C - 1 - np.arange(C)
            a[:, 1] = 0
            x[r] = a[:, rng.permutation(C) % 2]
        if o[r] % 4 == 3:
            l["co"][r] = rng.integers(0, K, (8, 1))
            x[r] = a[:, np.zeros(C, int)]
    return {"x": x.reshape(N, 128, 4 * C), "u": d["u"], "v": d["v"], **stored(l), **weights(rng, f(rng, N, 128, 2048))}
def setup_inputs_huge(rng):
    d, l = numbers_of(rng), lists_of(rng)
    o = rng.permutation(N)
    c = np.stack([rng.permutation(C) % 2 * 2.0 - 1.0 for r in range(N)])
    c[o == 0] = 1
    c[o == 1] = -1
    p = rng.random((N, 128, C, 4))
    x = np.where(c[:, None, :, None] < 0, -2.0 ** 30 * (1 - 0.125 * p), 2.0 ** 28 * (1 - 0.5 * p))
    k = np.stack([rng.permutation(8) % 4 for r in range(N)])
    s = 1.0 - 2.0 * np.stack([k >> 1, k & 1], axis=2)
    u = d["u"].reshape(N, 128, 8, 16, 4)
    a = 2.0 ** 30 * (1 - 0.25 * rng.random((N, 128, 8, 2, 4))) * s[:, None, :, :, None]
    u[:, :, :, :2] = a.astype(np.float32).astype(BF)
    w = np.zeros((N, 128, 4, 128, 4), np.float32)
    i = np.arange(128)
    for b in range(4): w[:, i, b, i, b] = 8
    return {"x": x.astype(np.float32).reshape(N, 128, 4 * C).astype(BF), "u": u.reshape(N, 128, 512), "v": d["v"], **stored(l), **weights(rng, w.reshape(N, 128, 2048).astype(BF))}
def setup_inputs_spread(rng):
    d = setup_inputs(rng)
    d["x"] = wide(rng, N, 128, 4 * C, cols=6)
    return d
def check_inputs(d):
    b = []
    for k in ("x", "u", "v"):
        a = np.abs(d[k].astype(np.float32))
        if not (np.isfinite(a).all() and ((a == 0) | (a >= 2.0 ** -30) & (a <= 2.0 ** 30)).all()): b.append("a value of " + k)
    if ((d["nx"] < 0) | (d["nx"] >= C)).any(): b.append("an entry of nx")
    if ((d["co"] < 0) | (d["co"] >= K)).any(): b.append("an entry of co")
    if ((d["wc"] == 0x7F) | (d["wc"] == 0xFF)).any(): b.append("a code of wc is no number")
    for r in range(N):
        s = mx_ref.live(d["ws"][r])
        if ((s > 1) & (s < 64) | (s > 191)).any(): b.append("a scale of ws")
    return b
def reference(x, u, v, nx, co, wc, ws):
    qu = [mx_ref.quantize(u[r]) for r in range(N)]
    lay = [pk(wc[r], ws[r]) for r in range(N)]
    now = [x[r] for r in range(N)]
    to = [gentries(nx[r]).astype(np.int64) for r in range(N)]
    cl = [gentries(co[r]).astype(np.int64) for r in range(N)]
    for t in range(R):
        held, sent = [], []
        for r in range(N):
            q = mx_ref.quantize(now[r])
            held.append(decode(q).astype(BF))
            neg = mx_ref.matmul(qu[r], q) + np.float32(0.0) < 0
            key = 4 * B * (cl[r] % A) + 4 * (np.take_along_axis(cl[r], to[r], axis=1) % B) + 2 * neg[::16] + neg[1::16]
            cl[r], one, two = classes(key)
            z = (gcols(held[r], one).astype(np.float32) + gcols(held[r], two).astype(np.float32)) * np.float32(0.5)
            sent.append(mx_ref.quantize(z.astype(BF)))
        for r in range(N):
            e = (r + STEP[t]) % N
            h = tile([np.maximum(mx_ref.matmul(pick(lay[e], np.arange(128 * b, 128 * b + 128)), sent[r]), np.float32(0.0)) * np.float32(0.03125) for b in range(4)])
            came = decode(mx_ref.quantize(h)).astype(BF)
            now[r] = (held[r].astype(np.float32) + gcols(came, cl[r]).astype(np.float32)).astype(BF)
    y, ol = np.zeros((N, 128, C), np.float32), np.zeros((N, 8, C), np.float32)
    oc, osc = np.zeros((N, 128, 4 * C), np.uint8), np.zeros((N, 16, C), np.uint8)
    for r in range(N):
        q = mx_ref.quantize(now[r])
        y[r] = mx_ref.matmul(mx_ref.quantize(v[r]), q)
        ol[r] = cl[r]
        oc[r], osc[r] = emit(q)
    return {"y": y, "ol": ol, "oc": oc, "osc": osc}

@@ -1,0 +1,484 @@
+import numpy as np
+from concourse.bass import DstId, RemoteDMATransfer
+from concourse.mybir import dt, AluOpType, ActivationFunctionType
+
+C, K, R = 224, 64, 3
+STEP = [1, 2, 4]
+W = 232
+XW = 304
+FW = 560
+D = 1.0 / 512
+L = 1.0 - D
+BF, F32, I32, U16, U8, MX = "bfloat16", "float32", "int32", "uint16", "uint8", "float8_e4m3fn_x4"
+
+
+def _sb(n, t):
+    return ("sbuf", [128, n], t)
+
+
+SCRATCH = {
+    "xt": _sb(896, BF), "ut": _sb(512, BF), "vt": _sb(512, BF), "nx32": _sb(16, I32), "co32": _sb(16, I32),
+    "wq": _sb(512, MX), "wsc": _sb(512, U8),
+    "qu": _sb(128, MX), "su": _sb(128, U8), "qab": _sb(256, MX), "sab": _sb(256, U8),
+    "qv": _sb(128, MX), "sv": _sb(128, U8), "qe": _sb(512, MX), "se": _sb(512, U8),
+    "qt": _sb(4 * C, MX), "st": _sb(4 * C, U8), "lq": _sb(3 * C, MX), "ls": _sb(3 * C, U8),
+    "qz": _sb(128, MX), "sz": _sb(128, U8), "qh": _sb(3 * 128, MX), "sh": _sb(3 * 128, U8),
+    "hq": _sb(3 * 192, MX), "hs": _sb(3 * 192, U8),
+    "tn": _sb(896, BF), "zt": _sb(512, BF), "ht": _sb(512, BF), "zero": _sb(512, BF), "eb": _sb(520, BF), "ones": _sb(128, BF),
+    "fh": _sb(4 * FW, BF), "fo": _sb(448, BF), "gd": _sb(256, BF), "zs": _sb(256, BF), "zk": _sb(256, BF), "ge": _sb(448, BF),
+    "yo": _sb(C, F32),
+    "lst": _sb(3 * 16, U16), "ll": _sb(3 * 16, U16), "nx16": _sb(16, U16), "co16": _sb(16, U16), "c16": _sb(16, U16),
+    "k16": _sb(16, U16), "p16": _sb(16, U16), "r16": _sb(4, U16), "u16": _sb(16, U16), "cd16": _sb(14, U16), "ct16": _sb(72, U16),
+    "ay": _sb(448, BF), "xr": _sb(3 * XW, BF), "cb": _sb(4 * W, BF), "so1": _sb(4 * W, BF), "so2": _sb(4 * W, BF),
+    "frv": _sb(64, F32), "junk": _sb(256, BF), "acc": _sb(4, F32), "srt": _sb(64, BF), "sol": _sb(64, BF),
+    "day": _sb(448, BF), "rk": _sb(64, BF), "r4": _sb(64, BF), "crow": _sb(C, BF), "crf": _sb(C, F32), "dc": _sb(C, BF),
+    "cm4": _sb(C, BF), "cm16": _sb(C, BF), "hb": _sb(240, BF), "dhp": _sb(C, BF), "dht": _sb(C, BF),
+    "h4": _sb(16, F32), "t1": _sb(16, F32), "t2": _sb(16, F32), "t3": _sb(16, F32), "t4": _sb(16, F32), "t5": _sb(16, F32),
+    "t6": _sb(16, F32), "ini": _sb(4, F32), "h0": _sb(1, F32),
+    "pi": _sb(1, I32), "ci": _sb(4, I32), "cf": _sb(4, F32), "col": _sb(12, F32), "r16f": _sb(16, F32), "kt": _sb(4, F32),
+    "mk": _sb(4, F32), "w1": _sb(72, F32), "w2": _sb(72, F32), "w3": _sb(72, F32), "w4": _sb(72, F32), "w5": _sb(72, F32),
+    "w6": _sb(72, F32), "w7": _sb(72, F32), "a36": _sb(36, F32), "b36": _sb(36, F32), "n36": _sb(72, F32), "d36": _sb(36, F32),
+    "t36": _sb(36, BF), "ctab": _sb(1152, BF), "e0": _sb(16, F32), "e1": _sb(16, F32), "wr": _sb(16, F32), "cds": _sb(16, BF),
+    "cd": _sb(C, BF), "m4": _sb(64, BF), "io": _sb(64, BF), "tv": _sb(296, F32),
+    "ps": ("psum", [128, 4096], F32),
+}
+LOADS = ["co", "nx", "x", "u", "wc", "ws", "v"]
+STORES = ["ol", "oc", "os0", "os1", "os2", "os3", "y"]
+SEMAPHORES = (["cV", "cS", "cP", "cG", "sent"] + ["d_" + n for n in LOADS + STORES]
+              + [a + str(t) for a in ("qarr", "larr", "karr", "harr") for t in range(R)])
+ADD, SUB, MUL, MAX, MIN = AluOpType.add, AluOpType.subtract, AluOpType.mult, AluOpType.max, AluOpType.min
+LT, EQ, NE = AluOpType.is_lt, AluOpType.is_equal, AluOpType.not_equal
+AND, SHR = AluOpType.bitwise_and, AluOpType.logical_shift_right
+AF = ActivationFunctionType
+
+
+def A(name, a=0, b=None, step=1, cast=None):
+    return ("ap", name, a, SCRATCH[name][1][1] if b is None else b, step, cast)
+
+
+def IND(win, off):
+    return ("ind", win, off)
+
+
+def bank(k, a=0, b=None):
+    return A("ps", 512 * k + a, 512 * k + (C if b is None else b))
+
+
+def _cells(v):
+    if v[0] == "ind":
+        return _cells(v[1]) + _cells(v[2])
+    m = np.zeros(SCRATCH[v[1]][1][1], bool)
+    if v[1] == "ps":
+        m[v[2] // 512 * 512:v[2] // 512 * 512 + 512] = True
+    else:
+        m[v[2]:v[3]:v[4]] = True
+    return [(v[1], m)]
+
+
+def rank_program(g, core, T, topo):
+    rank = T.rank_of(core)
+    if rank is None:
+        return
+    n = len(T.cores)
+    ops = []
+
+    def real(v):
+        if not isinstance(v, tuple):
+            return v
+        if v[0] == "ind":
+            return real(v[1]).indirect(real(v[2]))
+        r = T[v[1]][:, v[2]:v[3]] if v[4] == 1 else T[v[1]][:, v[2]:v[3]:v[4]]
+        return r if v[5] is None else r.bitcast(v[5])
+
+    def op(q, call, outs, ins, sem=None, val=0):
+        wr, rd = [], []
+        for v in outs:
+            if v[0] == "ind":
+                wr += _cells(v[1])
+                rd += _cells(v[2])
+            else:
+                wr += _cells(v)
+        for v in ins:
+            if isinstance(v, tuple):
+                for c in _cells(v):
+                    (wr if c[0] == "ps" else rd).append(c)
+        ops.append({"q": q, "call": call, "wr": wr, "rd": rd, "sem": sem, "val": val})
+
+    def ts(out, a, s1, op0, s2=None, op1=None):
+        if op1 is None:
+            op("V", lambda: g.vector.tensor_scalar(real(out), real(a), real(s1), None, op0), [out], [a, s1])
+        else:
+            op("V", lambda: g.vector.tensor_scalar(real(out), real(a), real(s1), real(s2), op0, op1), [out], [a, s1, s2])
+
+    def tt(out, a, b, o):
+        op("V", lambda: g.vector.tensor_tensor(real(out), real(a), real(b), o), [out], [a, b])
+
+    def cp(out, a):
+        op("V", lambda: g.vector.tensor_copy(real(out), real(a)), [out], [a])
+
+    def fill(out, c):
+        op("V", lambda: g.vector.memset(real(out), c), [out], [])
+
+    def scan(out, d0, d1, ini):
+        op("V", lambda: g.vector.tensor_tensor_scan(real(out), real(d0), real(d1), real(ini), ADD, MAX), [out], [d0, d1, ini])
+
+    def quant(q, s, a):
+        op("V", lambda: g.vector.quantize_mx(real(q), real(s), real(a)), [q, s], [a])
+
+    def act(out, a, f=AF.Copy, acc=None, **kw):
+        def call():
+            k = {x: real(y) for x, y in kw.items()}
+            if acc is not None:
+                k["accum_out"] = real(acc)
+            return g.scalar.activation(real(out), real(a), f, **k)
+        op("S", call, [out] + ([] if acc is None else [acc]), [a] + list(kw.values()))
+
+    def mm(out, wq, wsc, q, s):
+        op("P", lambda: g.tensor.matmul_mx(real(out), real(wq), real(wsc), real(q), real(s), True, True), [out], [wq, wsc, q, s])
+
+    def unpack(k, b, q, s, cols=C):
+        mm(bank(k, 0, cols), A("qe", 128 * b, 128 * b + 128), A("se", 128 * b, 128 * b + 128), q, s)
+
+    def iota(out, pat, base=0, cm=0):
+        if SCRATCH[out[1]][2] == I32:
+            op("G", lambda: g.iota(real(out), pat, base, cm), [out], [])
+        else:
+            op("G", lambda: g.iota(real(out), pat, base, cm, allow_small_or_imprecise_dtypes=True), [out], [])
+
+    def dma(q, name, dst, src, outs, ins):
+        e = g.sync if q == "Y" else g.scalar
+        op(q, lambda: e.dma_start(dst(), src()), outs, ins, sem="d_" + name, val=16)
+
+    sent = [0]
+
+    def send(to, dst, src, sem):
+        rid, pid = topo.addr(to, core)
+        sent[0] += len(topo.engines(core, to))
+        op("G", lambda: g.remote_dma(real(dst), real(src), T.sem[sem], T.sem["sent"], pid, rid, topo.mask(core, to)),
+           [], [src], sem="none")
+
+    def arrive(frm, calls, sem, outs):
+        op("X", None, outs, [], sem=sem, val=calls * len(topo.engines(frm, core)))
+
+    def u8(name, a, b):
+        return A(name, a, b, 1, dt.uint8)
+
+    def col(k):
+        return A("col", k, k + 1)
+
+    SIG, EPS, LAM, AA, AY, BETA, M17, Q1, BP, TMP = range(10)
+    icol, qcol, lacol, lbcol = [A("cf", k, k + 1) for k in range(4)]
+
+    dma("Y", "co", lambda: T["co32"][:, 0:14], lambda: T.co[:], [A("co32", 0, 14)], [])
+    dma("S", "x", lambda: T["xt"][:], lambda: T.x[:], [A("xt")], [])
+    dma("Y", "nx", lambda: T["nx32"][:, 0:14], lambda: T.nx[:], [A("nx32", 0, 14)], [])
+    dma("Y", "u", lambda: T["ut"][:], lambda: T.u[:], [A("ut")], [])
+    dma("Y", "wc", lambda: T["wq"][:].bitcast(dt.uint8), lambda: T.wc[:], [A("wq")], [A("nx32", 0, 14)])
+    dma("Y", "ws", lambda: T["wsc"][:], lambda: T.ws[:], [A("wsc")], [])
+
+    iota(A("pi"), [[1, 1]], 0, 1)
+    iota(A("w2"), [[-4, 4], [0, 18]])
+    iota(A("w1"), [[-4, 4], [1, 18]])
+    iota(A("a36"), [[1, 6], [0, 6]])
+    iota(A("b36"), [[0, 6], [1, 6]])
+    iota(A("r16f"), [[1, 16]])
+    iota(A("m4"), [[0, 16], [1, 4]])
+    fill(A("ones"), 1.0)
+    fill(A("eb"), 0.0)
+    for b in range(4):
+        act(A("fh", FW * b + C, FW * b + 256), A("eb", 0, 32))
+        act(A("fh", FW * b + 480, FW * b + FW), A("eb", 0, 80))
+    act(A("cb", 0, 4 * W, W), A("eb", 0, 4), AF.Identity, bias=D)
+    for s in range(1, 4):
+        act(A("cb", W * s + 225, W * s + 225 + s), A("eb", 0, s))
+    act(A("cb", 225, 4 * W, W + 1), A("eb", 0, 4), AF.Identity, bias=-2.0)
+    act(A("xr", 224, 3 * XW, XW), A("eb", 0, 3))
+    act(A("zt", 256, 512), A("eb", 0, 256))
+    ts(A("ci", 0, 1), A("pi"), 15, AND)
+    ts(A("ci", 1, 2), A("pi"), 2, SHR, 3, AND)
+    ts(A("ci", 2, 3), A("pi"), 1, SHR, 1, AND)
+    ts(A("ci", 3, 4), A("pi"), 1, AND)
+    cp(A("cf"), A("ci"))
+    ts(A("w3"), A("w1"), -1.0, MAX, 4.0, MIN)
+    ts(A("w5"), A("w2"), icol, ADD, -1.0, MAX)
+    ts(A("w4"), A("w3"), 6.0, MUL, 7.0, ADD)
+    ts(A("w6"), A("w5"), 4.0, MIN)
+    ts(col(Q1), qcol, 1.0, ADD)
+    tt(A("w7"), A("w4"), A("w6"), ADD)
+    ts(A("n36", 0, 36), A("a36"), col(Q1), NE)
+    ts(A("n36", 36, 72), A("b36"), col(Q1), NE)
+    cp(A("ct16"), A("w7"))
+    tt(A("d36"), A("n36", 0, 36), A("n36", 36, 72), SUB)
+    ts(A("wr"), A("r16f"), icol, SUB)
+    ts(A("t36"), A("d36"), L, MUL, D, ADD)
+    act(A("ctab", 0, 576), IND(A("t36"), A("ct16", 0, 36)))
+    act(A("ctab", 576, 1152), IND(A("t36"), A("ct16", 36, 72)))
+    op("G", lambda: g.affine_select(T["eb"][:, 3:515:4], T["ones"][:], [[1, 128]], EQ, 0.0, 0, -1), [A("eb", 3, 515, 4)], [A("ones")])
+    iota(A("tv"), [[-1, 296]], 223)
+    iota(A("io"), [[1, 64]])
+    ts(A("e0"), A("wr"), 0.0, EQ, -1024.0, MUL)
+    ts(A("e1"), A("wr"), 1.0, EQ, 64.0, MUL)
+    ts(A("cd16"), A("r16f", 0, 14), 0.0, MUL, icol, ADD)
+    ts(col(LAM), icol, 15.0, LT, 64.0, MUL)
+    tt(A("cds"), A("e0"), A("e1"), ADD)
+    ts(col(M17), icol, 15.0, LT, -17.0 * 64.0, MUL)
+    fill(A("hb", 224, 225), 16.0)
+    cp(A("cd"), IND(A("cds"), A("cd16")))
+    ts(A("u16", 0, 8), A("r16f", 0, 8), 16.0, MUL)
+    ts(A("u16", 8, 16), A("r16f", 0, 8), 16.0, MUL, 1.0, ADD)
+    ts(A("kt"), A("r16f", 0, 4), 4.0, MUL, qcol, ADD)
+    ts(col(SIG), lbcol, -2.0, MUL, 1.0, ADD)
+
+    def send_state(t):
+        to = T.cores[(rank + STEP[t]) % n]
+        send(to, u8("lq", C * t, C * t + C), u8("qt", C * t, C * t + C), "qarr%d" % t)
+        send(to, A("ls", C * t, C * t + C), A("st", C * t, C * t + C), "qarr%d" % t)
+
+    def step_row(s):
+        act(A("cb", W * s + 1, W * s + 1 + C), IND(A("ctab", 288 * s, 288 * s + 288), A("p16", 0, 14)))
+
+    def high_a():
+        ts(A("cm16"), A("cm4"), 4.0, MUL)
+
+    def high_b():
+        tt(A("hb", 0, C), IND(A("cm4"), A("nx16", 0, 14)), A("cm16"), ADD)
+
+    def high_c():
+        scan(A("dht"), A("cd"), A("hb", 1, C + 1), 0.0)
+        scan(A("dhp"), A("cd"), A("hb", 0, C), 0.0)
+        ts(A("t5", 0, 14), A("dht", 15, C, 16), 16.0, MUL, col(M17), ADD)
+        cp(A("h0"), A("hb", 0, 1))
+        tt(A("t6", 0, 14), A("t5", 0, 14), A("dhp", 15, C, 16), ADD)
+        ts(A("ini"), A("kt"), A("h0"), NE, L, MUL)
+        cp(A("p16", 0, 14), A("t6", 0, 14))
+        ts(A("h4", 0, 14), A("dhp", 15, C, 16), col(LAM), SUB, 4.0, MUL)
+
+    def unit(b):
+        quant(A("qe", 128 * b, 128 * b + 128), A("se", 128 * b, 128 * b + 128), A("eb", 3 - b, 515 - b))
+
+    def pad(t):
+        quant(A("hq", 192 * t, 192 * t + 128), A("hs", 192 * t, 192 * t + 128), A("zero"))
+
+    def marks(t):
+        ts(A("xr", XW * t + 225, XW * t + 229), A("mk"), 6.0, ADD, -D, MUL)
+
+    cp(A("co16", 0, 14), A("co32", 0, 14))
+    cp(A("nx16", 0, 14), A("nx32", 0, 14))
+    cp(A("cm4"), IND(A("m4"), A("co16", 0, 14)))
+    act(A("zero"), A("eb", 0, 512), AF.Identity, scale=0.0)
+    quant(A("qt", 0, C), A("st", 0, C), A("xt"))
+    high_a()
+    send_state(0)
+    quant(A("qu"), A("su"), A("ut"))
+    high_b()
+    act(A("sab"), IND(A("su"), A("u16")))
+    act(A("ht", 256, 512), A("zero", 0, 256))
+    high_c()
+    step_row(0)
+    step_row(1)
+    cp(A("qab", 0, 256, 1, dt.uint32), IND(A("qu", 0, 128, 1, dt.uint32), A("u16")))
+    ts(col(EPS), col(SIG), 2.0 ** -120, MUL)
+    ts(A("mk"), A("r16f", 0, 4), 16.0, MUL, icol, ADD)
+
+    for t in range(R):
+        last = t == R - 1
+        to = T.cores[(rank + STEP[t]) % n]
+        frm = T.cores[(rank - STEP[t]) % n]
+        qt, st = A("qt", C * t, C * t + C), A("st", C * t, C * t + C)
+        x0, l0 = XW * t, 16 * t
+        mm(bank(0), A("qab", 0, 128), A("sab", 0, 128), qt, st)
+        mm(bank(1), A("qab", 128, 256), A("sab", 128, 256), qt, st)
+        if t == 0:
+            marks(0)
+            unit(0)
+        else:
+            pad(t)
+        ts(A("ay", 0, C), bank(0), 0.0, LT, lacol, EQ)
+        act(A("ay", C, 2 * C), bank(1), AF.Sign, scale=col(SIG), bias=col(EPS))
+        if t == 0:
+            step_row(2)
+            step_row(3)
+            unit(1)
+        else:
+            scan(A("day", 0, C), A("cd"), A("ay", 0, C), 0.0)
+        tt(A("xr", x0, x0 + C), A("ay", 0, C), A("ay", C, 2 * C), MUL)
+        for s in range(4):
+            scan(A("so1", W * s, W * s + 226 + s), A("cb", W * s, W * s + 226 + s), A("xr", x0, x0 + 226 + s), A("ini", s, s + 1))
+        fin1 = A("so1", 225, 4 * W, W + 1)
+        f16 = A("lst", l0, l0 + 4)
+        ts(f16, fin1, -512.0, MUL, 223.0, ADD)
+        act(A("xr", x0 + 225, x0 + 229), fin1, AF.Identity, bias=-0.5)
+        cp(IND(A("xr", x0, x0 + 293), f16), A("zero", 0, 64))
+        act(A("frv"), IND(A("tv", 0, 293), f16))
+        for s in range(4):
+            act(A("junk", 64 * s, 64 * s + 64), A("frv"), AF.Sign, acc=A("acc", s, s + 1), scale=-D,
+                bias=A("so1", (W + 1) * s + 225, (W + 1) * s + 226))
+        for s in range(4):
+            scan(A("so2", W * s, W * s + 226 + s), A("cb", W * s, W * s + 226 + s), A("xr", x0, x0 + 226 + s), A("ini", s, s + 1))
+        ts(A("lst", l0 + 4, l0 + 8), A("so2", 225, 4 * W, W + 1), -512.0, MUL, 223.0, ADD)
+        send(to, A("ll", l0, l0 + 8), A("lst", l0, l0 + 8), "larr%d" % t)
+        ts(A("r16"), A("acc"), -0.5, MUL, 31.5, ADD)
+        cp(IND(A("srt"), A("r16")), A("io"))
+        scan(A("sol"), A("cd", 0, 64), A("srt"), 0.0)
+        ts(A("lst", l0 + 8, l0 + 12), A("sol", 15, 64, 16), col(LAM), SUB)
+        send(to, A("ll", l0 + 8, l0 + 12), A("lst", l0 + 8, l0 + 12), "karr%d" % t)
+        lq, ls = A("lq", C * t, C * t + C), A("ls", C * t, C * t + C)
+        arrive(frm, 2, "qarr%d" % t, [lq, ls])
+        if t == 0:
+            unit(2)
+            unit(3)
+        act(A("rk"), IND(A("io"), A("r16")))
+        for b in range(4):
+            unpack(4 + b, b, lq, ls)
+        for b in (0, 2):
+            act(A("fh", FW * b, FW * b + C), bank(4 + b), AF.Identity, scale=0.5)
+        act(A("fh", FW * 2 + 256, FW * 2 + 256 + C), bank(6), AF.Identity, scale=0.5)
+
+        def half(b):
+            ts(A("fh", FW * b, FW * b + C), bank(4 + b), 0.5, MUL)
+
+        def again(b):
+            cp(A("fh", FW * b + 256, FW * b + 256 + C), A("fh", FW * b, FW * b + C))
+
+        if t == 0:
+            ts(col(AA), lacol, 4.0, MUL, -2.0, ADD)
+            ts(col(AY), col(SIG), -0.5, MUL)
+            ts(col(BP), lacol, -2.0, MUL, 2.5, ADD)
+            scan(A("day", 0, C), A("cd"), A("ay", 0, C), 0.0)
+            ts(col(TMP), col(AA), col(AY), ADD, col(LAM), MUL)
+        scan(A("day", C, 2 * C), A("cd"), A("ay", C, 2 * C), 0.0)
+        if t == 0:
+            ts(col(BETA), col(BP), col(TMP), SUB)
+        ts(A("t2", 0, 14), A("day", C + 15, 2 * C, 16), col(AY), MUL)
+        ts(A("t1", 0, 14), A("day", 15, C, 16), col(AA), MUL, col(BETA), ADD)
+        tt(A("t3", 0, 14), A("t2", 0, 14), A("h4", 0, 14), ADD)
+        half(1)
+        again(0)
+        tt(A("t4", 0, 14), A("t3", 0, 14), A("t1", 0, 14), ADD)
+        half(3)
+        again(1)
+        cp(A("k16", 0, 14), A("t4", 0, 14))
+        again(3)
+        arrive(frm, 1, "larr%d" % t, [A("ll", l0, l0 + 8)])
+        arrive(frm, 1, "karr%d" % t, [A("ll", l0 + 8, l0 + 12)])
+        sec = [IND(A("fh", FW * b, FW * b + FW), A("ll", l0 + 4, l0 + 8)) for b in range(4)]
+        cp(A("zs", 0, 64), sec[0])
+        for b in range(1, 4):
+            act(A("zs", 64 * b, 64 * b + 64), sec[b])
+        for b in range(4):
+            tt(A("zk", 64 * b, 64 * b + 64), IND(A("fh", FW * b + 256, FW * b + FW), A("ll", l0, l0 + 4)), A("zs", 64 * b, 64 * b + 64), ADD)
+        for b in range(4):
+            (act if b < 2 else cp)(A("zt", b, 256, 4), IND(A("zk", 64 * b, 64 * b + 64), A("ll", l0 + 8, l0 + 12)))
+        quant(A("qz"), A("sz"), A("zt"))
+        for b in range(4):
+            mm(bank(b, 0, 128), A("wq", 128 * b, 128 * b + 128), A("wsc", 128 * b, 128 * b + 128), A("qz"), A("sz"))
+        if last:
+            quant(A("qv"), A("sv"), A("vt"))
+        else:
+            cp(A("r4"), IND(A("m4"), A("r16")))
+            marks(t + 1)
+        for b in range(4):
+            if b % 2 == 0:
+                act(A("ht", b, 256, 4), bank(b, 0, 64), AF.Relu, scale=0.03125)
+            else:
+                ts(A("ht", b, 256, 4), bank(b, 0, 64), 0.0, MAX, 0.03125, MUL)
+        h0, h1 = 128 * t, 192 * t
+        quant(A("qh", h0, h0 + 128), A("sh", h0, h0 + 128), A("ht"))
+        send(frm, u8("hq", h1 + 128, h1 + 192), u8("qh", h0, h0 + 64), "harr%d" % t)
+        send(frm, A("hs", h1 + 128, h1 + 192), A("sh", h0, h0 + 64), "harr%d" % t)
+        for b in range(4):
+            unpack(4 + b, b, qt, st)
+        cr = A("crf") if last else A("crow")
+        act(cr, IND(A("rk"), A("k16", 0, 14)))
+        for b in range(2):
+            act(A("fo", C * b, C * b + C), bank(4 + b))
+        if t == 0:
+            pad(0)
+        if not last:
+            cp(A("cm4"), IND(A("r4"), A("k16", 0, 14)))
+        scan(A("dc"), A("cd"), cr, 0.0)
+        if not last:
+            high_a()
+        ts(A("c16", 0, 14), A("dc", 15, C, 16), col(LAM), SUB)
+        if not last:
+            high_b()
+            high_c()
+            step_row(0)
+            step_row(1)
+        arrive(to, 2, "harr%d" % t, [A("hq", h1 + 128, h1 + 192), A("hs", h1 + 128, h1 + 192)])
+        for b in range(4):
+            unpack(b, b, A("hq", h1 + 64, h1 + 192), A("hs", h1 + 64, h1 + 192), 128)
+        for b in range(4):
+            (cp if b < 2 else act)(A("gd", 64 * b, 64 * b + 64), bank(b, 64, 128))
+        if t == 0:
+            dma("Y", "v", lambda: T["vt"][:], lambda: T.v[:], [A("vt")], [A("gd", 0, 64)])
+        if last:
+            dma("Y", "ol", lambda: T.ol[:], lambda: T["crf"][0:128:16, :], [], [cr, A("c16", 0, 14)])
+        cl = A("c16", 0, 14)
+        for b in range(2):
+            tt(A("tn", b, 896, 4), IND(A("gd", 64 * b, 64 * b + 64), cl), A("fo", C * b, C * b + C), ADD)
+        for b in range(2, 4):
+            act(A("ge", C * (b - 2), C * (b - 1)), IND(A("gd", 64 * b, 64 * b + 64), cl))
+        for b in range(2, 4):
+            tt(A("tn", b, 896, 4), A("ge", C * (b - 2), C * (b - 1)), bank(4 + b), ADD)
+        quant(A("qt", C * t + C, C * t + 2 * C), A("st", C * t + C, C * t + 2 * C), A("tn"))
+        if not last:
+            send_state(t + 1)
+            step_row(2)
+            step_row(3)
+
+    q0 = R * C
+    mm(bank(0, 0, 128), A("qv"), A("sv"), A("qt", q0, q0 + 128), A("st", q0, q0 + 128))
+    mm(bank(1, 0, 128), A("qv"), A("sv"), A("qt", q0 + 96, q0 + C), A("st", q0 + 96, q0 + C))
+    cp(A("yo", 0, 128), bank(0, 0, 128))
+    act(A("yo", 128, C), bank(1, 32, 128))
+    dma("Y", "oc", lambda: T.oc[:], lambda: T["qt"][:, q0:q0 + C].bitcast(dt.uint8), [], [A("qt", q0, q0 + C)])
+    dma("S", "y", lambda: T.y[:], lambda: T["yo"][:], [], [A("yo")])
+    for k in range(4):
+        dma("Y", "os%d" % k, lambda k=k: T.osc[4 * k:4 * k + 4, :], lambda k=k: T["st"][32 * k:32 * k + 4, q0:q0 + C],
+            [], [A("st", q0, q0 + C)])
+
+    seen, known, waited = {}, {q: set() for q in "VSPGY"}, set()
+    last_on = {}
+    for i, o in enumerate(ops):
+        deps = set()
+        for name, m in o["wr"]:
+            deps |= {j for j, mj, w in seen.get(name, []) if (m & mj).any()}
+        for name, m in o["rd"]:
+            deps |= {j for j, mj, w in seen.get(name, []) if w and (m & mj).any()}
+        for name, m in o["wr"]:
+            seen.setdefault(name, []).append((i, m, True))
+        for name, m in o["rd"]:
+            seen.setdefault(name, []).append((i, m, False))
+        deps.discard(i)
+        o["waits"] = []
+        if o["q"] == "X":
+            o["done"] = {i}
+            continue
+        kn = known[o["q"]]
+        for j in sorted(deps, reverse=True):
+            if j not in kn:
+                o["waits"].append(j)
+                waited.add(j)
+                kn |= ops[j]["done"]
+        o["done"] = set(kn) | {i}
+        if o["sem"] is None:
+            o["done"] |= last_on.get(o["q"], set())
+            last_on[o["q"]] = o["done"]
+    count = {q: 0 for q in "VSPG"}
+    for i, o in enumerate(ops):
+        if o["sem"] is None and i in waited:
+            count[o["q"]] += 1
+            o["sem"], o["val"], o["inc"] = "c" + o["q"], count[o["q"]], 1
+    queue = {"V": g.vector, "S": g.scalar, "P": g.tensor, "G": g, "Y": g.sync}
+    for i, o in enumerate(ops):
+        if o["q"] == "X":
+            continue
+        for j in o["waits"]:
+            queue[o["q"]].wait_ge(T.sem[ops[j]["sem"]], ops[j]["val"])
+        ins = o["call"]()
+        if o["sem"] is not None and o["sem"] != "none":
+            ins.then_inc(T.sem[o["sem"]], o.get("inc", 16))
+    g.wait_ge(T.sem["sent"], sent[0])
+    for name in STORES:
+        g.wait_ge(T.sem["d_" + name], 16)

@@ -4,9 +4,9 @@ from concourse.mybir import dt, AluOpType, ActivationFunctionType
 
 C, K, R = 224, 64, 3
 STEP = [1, 2, 4]
-W = 232
-XW = 304
-FW = 560
+W = 244
+N1, N2 = 227, 228
+FW = 512
 D = 1.0 / 512
 L = 1.0 - D
 BF, F32, I32, U16, U8, MX = "bfloat16", "float32", "int32", "uint16", "uint8", "float8_e4m3fn_x4"
@@ -23,23 +23,24 @@ SCRATCH = {
     "qv": _sb(128, MX), "sv": _sb(128, U8), "qe": _sb(512, MX), "se": _sb(512, U8),
     "qt": _sb(4 * C, MX), "st": _sb(4 * C, U8), "lq": _sb(3 * C, MX), "ls": _sb(3 * C, U8),
     "qz": _sb(128, MX), "sz": _sb(128, U8), "qh": _sb(3 * 128, MX), "sh": _sb(3 * 128, U8),
-    "hq": _sb(3 * 192, MX), "hs": _sb(3 * 192, U8),
-    "tn": _sb(896, BF), "zt": _sb(512, BF), "ht": _sb(512, BF), "zero": _sb(512, BF), "eb": _sb(520, BF), "ones": _sb(128, BF),
+    "hq": _sb(128 + 3 * K, MX), "hs": _sb(128 + 3 * K, U8),
+    "tn": _sb(896, BF), "zt": _sb(512, BF), "ht": _sb(512, BF), "zero": _sb(512, BF), "eb": _sb(520, BF), "ones": _sb(288, BF),
     "fh": _sb(4 * FW, BF), "fo": _sb(448, BF), "gd": _sb(256, BF), "zs": _sb(256, BF), "zk": _sb(256, BF), "ge": _sb(448, BF),
     "yo": _sb(C, F32),
     "lst": _sb(3 * 16, U16), "ll": _sb(3 * 16, U16), "nx16": _sb(16, U16), "co16": _sb(16, U16), "c16": _sb(16, U16),
-    "k16": _sb(16, U16), "p16": _sb(16, U16), "r16": _sb(4, U16), "u16": _sb(16, U16), "cd16": _sb(14, U16), "ct16": _sb(72, U16),
-    "ay": _sb(448, BF), "xr": _sb(3 * XW, BF), "cb": _sb(4 * W, BF), "so1": _sb(4 * W, BF), "so2": _sb(4 * W, BF),
-    "frv": _sb(64, F32), "junk": _sb(256, BF), "acc": _sb(4, F32), "srt": _sb(64, BF), "sol": _sb(64, BF),
-    "day": _sb(448, BF), "rk": _sb(64, BF), "r4": _sb(64, BF), "crow": _sb(C, BF), "crf": _sb(C, F32), "dc": _sb(C, BF),
-    "cm4": _sb(C, BF), "cm16": _sb(C, BF), "hb": _sb(240, BF), "dhp": _sb(C, BF), "dht": _sb(C, BF),
-    "h4": _sb(16, F32), "t1": _sb(16, F32), "t2": _sb(16, F32), "t3": _sb(16, F32), "t4": _sb(16, F32), "t5": _sb(16, F32),
-    "t6": _sb(16, F32), "ini": _sb(4, F32), "h0": _sb(1, F32),
-    "pi": _sb(1, I32), "ci": _sb(4, I32), "cf": _sb(4, F32), "col": _sb(12, F32), "r16f": _sb(16, F32), "kt": _sb(4, F32),
+    "k16": _sb(16, U16), "p16": _sb(16, U16), "r16": _sb(4, U16), "u16": _sb(16, U16), "cd16": _sb(16, U16), "ct16": _sb(72, U16),
+    "ya": _sb(C, BF), "yb": _sb(C, BF), "z1": _sb(C, BF), "xv": _sb(W, BF), "cb": _sb(4 * W, BF), "so1": _sb(4 * W, BF),
+    "d2": _sb(4 * W, BF), "so2": _sb(4 * W, BF), "in1": _sb(4, F32), "in2": _sb(4, F32),
+    "frv": _sb(64, BF), "junk": _sb(256, BF), "acc": _sb(4, F32), "srt": _sb(64, BF), "sol": _sb(64, BF),
+    "da": _sb(C, BF), "db": _sb(C, BF), "rk": _sb(64, BF), "r4": _sb(64, BF), "crow": _sb(C, BF), "crf": _sb(C, F32), "dc": _sb(C, BF),
+    "cm4": _sb(C, BF), "cm16": _sb(C, BF), "hb": _sb(W, BF), "dh": _sb(240, BF), "dp": _sb(240, BF),
+    "cdp": _sb(240, BF), "cda": _sb(240, BF), "cdb": _sb(240, BF),
+    "pi": _sb(1, I32), "ci": _sb(4, I32), "cf": _sb(4, F32), "col": _sb(16, F32), "r16f": _sb(16, F32), "kt": _sb(4, F32),
     "mk": _sb(4, F32), "w1": _sb(72, F32), "w2": _sb(72, F32), "w3": _sb(72, F32), "w4": _sb(72, F32), "w5": _sb(72, F32),
     "w6": _sb(72, F32), "w7": _sb(72, F32), "a36": _sb(36, F32), "b36": _sb(36, F32), "n36": _sb(72, F32), "d36": _sb(36, F32),
-    "t36": _sb(36, BF), "ctab": _sb(1152, BF), "e0": _sb(16, F32), "e1": _sb(16, F32), "wr": _sb(16, F32), "cds": _sb(16, BF),
-    "cd": _sb(C, BF), "m4": _sb(64, BF), "io": _sb(64, BF), "tv": _sb(296, F32),
+    "t36": _sb(36, BF), "ctab": _sb(1152, BF), "e0": _sb(16, F32), "e1": _sb(16, F32), "e2": _sb(16, F32), "e3": _sb(16, F32),
+    "wr": _sb(16, F32), "cds": _sb(16, BF), "cd": _sb(240, BF), "m4": _sb(64, BF), "io": _sb(64, BF), "tv": _sb(288, BF),
+    "place": _sb(C, BF),
     "ps": ("psum", [128, 4096], F32),
 }
 LOADS = ["co", "nx", "x", "u", "wc", "ws", "v"]
@@ -47,7 +48,7 @@ STORES = ["ol", "oc", "os0", "os1", "os2", "os3", "y"]
 SEMAPHORES = (["cV", "cS", "cP", "cG", "sent"] + ["d_" + n for n in LOADS + STORES]
               + [a + str(t) for a in ("qarr", "larr", "karr", "harr") for t in range(R)])
 ADD, SUB, MUL, MAX, MIN = AluOpType.add, AluOpType.subtract, AluOpType.mult, AluOpType.max, AluOpType.min
-LT, EQ, NE = AluOpType.is_lt, AluOpType.is_equal, AluOpType.not_equal
+GT, EQ, NE = AluOpType.is_gt, AluOpType.is_equal, AluOpType.not_equal
 AND, SHR = AluOpType.bitwise_and, AluOpType.logical_shift_right
 AF = ActivationFunctionType
 
@@ -119,8 +120,11 @@ def rank_program(g, core, T, topo):
     def fill(out, c):
         op("V", lambda: g.vector.memset(real(out), c), [out], [])
 
-    def scan(out, d0, d1, ini):
-        op("V", lambda: g.vector.tensor_tensor_scan(real(out), real(d0), real(d1), real(ini), ADD, MAX), [out], [d0, d1, ini])
+    def scan(out, d0, d1, ini, op0=ADD, op1=MAX):
+        op("V", lambda: g.vector.tensor_tensor_scan(real(out), real(d0), real(d1), real(ini), op0, op1), [out], [d0, d1, ini])
+
+    def hold(out, row, steps):
+        scan(out, row, steps, -2.0, MAX, ADD)
 
     def quant(q, s, a):
         op("V", lambda: g.vector.quantize_mx(real(q), real(s), real(a)), [q, s], [a])
@@ -166,8 +170,9 @@ def rank_program(g, core, T, topo):
     def col(k):
         return A("col", k, k + 1)
 
-    SIG, EPS, LAM, AA, AY, BETA, M17, Q1, BP, TMP = range(10)
+    SGA, SGB, EPA, EPB, Q1, PC, A0, A1, B0, B1, K0, K1 = range(12)
     icol, qcol, lacol, lbcol = [A("cf", k, k + 1) for k in range(4)]
+    end = A("cds", 15, 16)
 
     dma("Y", "co", lambda: T["co32"][:, 0:14], lambda: T.co[:], [A("co32", 0, 14)], [])
     dma("S", "x", lambda: T["xt"][:], lambda: T.x[:], [A("xt")], [])
@@ -181,236 +186,306 @@ def rank_program(g, core, T, topo):
     iota(A("w1"), [[-4, 4], [1, 18]])
     iota(A("a36"), [[1, 6], [0, 6]])
     iota(A("b36"), [[0, 6], [1, 6]])
-    iota(A("r16f"), [[1, 16]])
     iota(A("m4"), [[0, 16], [1, 4]])
     fill(A("ones"), 1.0)
     fill(A("eb"), 0.0)
-    for b in range(4):
-        act(A("fh", FW * b + C, FW * b + 256), A("eb", 0, 32))
-        act(A("fh", FW * b + 480, FW * b + FW), A("eb", 0, 80))
-    act(A("cb", 0, 4 * W, W), A("eb", 0, 4), AF.Identity, bias=D)
-    for s in range(1, 4):
-        act(A("cb", W * s + 225, W * s + 225 + s), A("eb", 0, s))
-    act(A("cb", 225, 4 * W, W + 1), A("eb", 0, 4), AF.Identity, bias=-2.0)
-    act(A("xr", 224, 3 * XW, XW), A("eb", 0, 3))
-    act(A("zt", 256, 512), A("eb", 0, 256))
+    fill(A("xv"), -1.0)
+    fill(A("hb"), 0.0)
+    scan(A("tv"), A("ones"), A("ones"), -127.0, ADD, MUL)
     ts(A("ci", 0, 1), A("pi"), 15, AND)
     ts(A("ci", 1, 2), A("pi"), 2, SHR, 3, AND)
     ts(A("ci", 2, 3), A("pi"), 1, SHR, 1, AND)
     ts(A("ci", 3, 4), A("pi"), 1, AND)
+    ts(A("r16f"), A("tv", 0, 16), 126.0, ADD)
+    fill(A("hb", 225, 227), 16.0)
     cp(A("cf"), A("ci"))
+    act(A("zero"), A("eb", 0, 512))
+    for b in range(4):
+        act(A("fh", FW * b + 2 * C, FW * b + FW), A("eb", 0, 64))
+    act(A("d2", 0, 4 * W, W), A("eb", 0, 4), AF.Identity, bias=-2.0)
+    for k in range(225, 228):
+        act(A("d2", k, 4 * W, W), A("eb", 0, 4), AF.Identity, bias=-2.0)
     ts(A("w3"), A("w1"), -1.0, MAX, 4.0, MIN)
+    fill(A("hb", 227, 228), 16.25)
     ts(A("w5"), A("w2"), icol, ADD, -1.0, MAX)
-    ts(A("w4"), A("w3"), 6.0, MUL, 7.0, ADD)
-    ts(A("w6"), A("w5"), 4.0, MIN)
     ts(col(Q1), qcol, 1.0, ADD)
-    tt(A("w7"), A("w4"), A("w6"), ADD)
+    ts(A("w4"), A("w3"), 6.0, MUL, 7.0, ADD)
+    ts(A("wr"), A("r16f"), icol, SUB)
+    ts(A("w6"), A("w5"), 4.0, MIN)
     ts(A("n36", 0, 36), A("a36"), col(Q1), NE)
     ts(A("n36", 36, 72), A("b36"), col(Q1), NE)
-    cp(A("ct16"), A("w7"))
+    ts(A("e0"), A("wr"), -1.0, EQ, -256.0, MUL)
+    tt(A("w7"), A("w4"), A("w6"), ADD)
+    ts(A("e1"), A("wr"), 0.0, EQ, 64.0, MUL)
     tt(A("d36"), A("n36", 0, 36), A("n36", 36, 72), SUB)
-    ts(A("wr"), A("r16f"), icol, SUB)
+    ts(A("e2"), A("r16f"), 15.0, EQ, -128.0, MUL)
+    cp(A("ct16"), A("w7"))
+    tt(A("e3"), A("e0"), A("e1"), ADD)
     ts(A("t36"), A("d36"), L, MUL, D, ADD)
+    ts(A("cd16"), A("r16f"), 0.0, MUL, icol, ADD)
+    ts(col(SGA), lacol, -2.0, MUL, 1.0, ADD)
+    tt(A("cds"), A("e3"), A("e2"), ADD)
     act(A("ctab", 0, 576), IND(A("t36"), A("ct16", 0, 36)))
     act(A("ctab", 576, 1152), IND(A("t36"), A("ct16", 36, 72)))
-    op("G", lambda: g.affine_select(T["eb"][:, 3:515:4], T["ones"][:], [[1, 128]], EQ, 0.0, 0, -1), [A("eb", 3, 515, 4)], [A("ones")])
-    iota(A("tv"), [[-1, 296]], 223)
-    iota(A("io"), [[1, 64]])
-    ts(A("e0"), A("wr"), 0.0, EQ, -1024.0, MUL)
-    ts(A("e1"), A("wr"), 1.0, EQ, 64.0, MUL)
-    ts(A("cd16"), A("r16f", 0, 14), 0.0, MUL, icol, ADD)
-    ts(col(LAM), icol, 15.0, LT, 64.0, MUL)
-    tt(A("cds"), A("e0"), A("e1"), ADD)
-    ts(col(M17), icol, 15.0, LT, -17.0 * 64.0, MUL)
-    fill(A("hb", 224, 225), 16.0)
-    cp(A("cd"), IND(A("cds"), A("cd16")))
+    op("G", lambda: g.affine_select(T["eb"][:, 3:515:4], T["ones"][:, 0:128], [[1, 128]], EQ, 0.0, 0, -1),
+       [A("eb", 3, 515, 4)], [A("ones", 0, 128)])
     ts(A("u16", 0, 8), A("r16f", 0, 8), 16.0, MUL)
     ts(A("u16", 8, 16), A("r16f", 0, 8), 16.0, MUL, 1.0, ADD)
-    ts(A("kt"), A("r16f", 0, 4), 4.0, MUL, qcol, ADD)
-    ts(col(SIG), lbcol, -2.0, MUL, 1.0, ADD)
+    cp(A("cd"), IND(A("cds"), A("cd16", 0, 15)))
 
     def send_state(t):
         to = T.cores[(rank + STEP[t]) % n]
         send(to, u8("lq", C * t, C * t + C), u8("qt", C * t, C * t + C), "qarr%d" % t)
         send(to, A("ls", C * t, C * t + C), A("st", C * t, C * t + C), "qarr%d" % t)
 
-    def step_row(s):
-        act(A("cb", W * s + 1, W * s + 1 + C), IND(A("ctab", 288 * s, 288 * s + 288), A("p16", 0, 14)))
+    def step_row(s, on):
+        on(A("cb", W * s + 1, W * s + 241), IND(A("ctab", 288 * s, 288 * s + 288), A("p16", 0, 15)))
 
-    def high_a():
-        ts(A("cm16"), A("cm4"), 4.0, MUL)
+    def high_row():
+        tt(A("hb", 1, C + 1), IND(A("cm4"), A("nx16", 0, 14)), A("cm16"), ADD)
 
-    def high_b():
-        tt(A("hb", 0, C), IND(A("cm4"), A("nx16", 0, 14)), A("cm16"), ADD)
+    def high_hold():
+        hold(A("dh"), A("hb", 1, 241), A("cd"))
 
-    def high_c():
-        scan(A("dht"), A("cd"), A("hb", 1, C + 1), 0.0)
-        scan(A("dhp"), A("cd"), A("hb", 0, C), 0.0)
-        ts(A("t5", 0, 14), A("dht", 15, C, 16), 16.0, MUL, col(M17), ADD)
-        cp(A("h0"), A("hb", 0, 1))
-        tt(A("t6", 0, 14), A("t5", 0, 14), A("dhp", 15, C, 16), ADD)
-        ts(A("ini"), A("kt"), A("h0"), NE, L, MUL)
-        cp(A("p16", 0, 14), A("t6", 0, 14))
-        ts(A("h4", 0, 14), A("dhp", 15, C, 16), col(LAM), SUB, 4.0, MUL)
+    def high_steps():
+        ts(A("cdp", 15, 240, 16), A("dh", 15, 240, 16), 16.0, MUL, col(PC), ADD)
+
+    def key_steps():
+        ts(A("cda", 15, C, 16), A("dh", 15, C, 16), col(A0), MUL, col(A1), ADD)
+
+    def pair_hold():
+        hold(A("dp"), A("hb", 0, 240), A("cdp"))
+
+    def pair_list():
+        ts(A("p16", 0, 15), A("dp", 15, 240, 16), 256.0, ADD)
 
     def unit(b):
         quant(A("qe", 128 * b, 128 * b + 128), A("se", 128 * b, 128 * b + 128), A("eb", 3 - b, 515 - b))
 
-    def pad(t):
-        quant(A("hq", 192 * t, 192 * t + 128), A("hs", 192 * t, 192 * t + 128), A("zero"))
-
-    def marks(t):
-        ts(A("xr", XW * t + 225, XW * t + 229), A("mk"), 6.0, ADD, -D, MUL)
-
     cp(A("co16", 0, 14), A("co32", 0, 14))
     cp(A("nx16", 0, 14), A("nx32", 0, 14))
+    ts(col(PC), end, 832.0, ADD)
     cp(A("cm4"), IND(A("m4"), A("co16", 0, 14)))
-    act(A("zero"), A("eb", 0, 512), AF.Identity, scale=0.0)
     quant(A("qt", 0, C), A("st", 0, C), A("xt"))
-    high_a()
+    ts(A("cm16"), A("cm4"), 4.0, MUL)
     send_state(0)
     quant(A("qu"), A("su"), A("ut"))
-    high_b()
+    high_row()
     act(A("sab"), IND(A("su"), A("u16")))
-    act(A("ht", 256, 512), A("zero", 0, 256))
-    high_c()
-    step_row(0)
-    step_row(1)
+    cp(A("cdp"), A("cd"))
+    high_hold()
+    ts(col(SGB), lbcol, -2.0, MUL, 1.0, ADD)
+    ts(col(EPA), col(SGA), 2.0 ** -120, MUL)
+    high_steps()
     cp(A("qab", 0, 256, 1, dt.uint32), IND(A("qu", 0, 128, 1, dt.uint32), A("u16")))
-    ts(col(EPS), col(SIG), 2.0 ** -120, MUL)
+    pair_hold()
+    ts(col(EPB), col(SGB), 2.0 ** -120, MUL)
+    fill(A("ctab", 272, 1152, 288), -1.3125)
+    fill(A("ctab", 276, 1152, 288), -0.625)
+    pair_list()
+    ts(A("place"), A("tv", 0, C), 126.0, ADD, 1.0 / 1024, MUL)
+    ts(A("kt"), A("r16f", 0, 4), 4.0, MUL, qcol, ADD)
     ts(A("mk"), A("r16f", 0, 4), 16.0, MUL, icol, ADD)
+    step_row(0, cp)
+    step_row(2, act)
+    ts(A("cb", 0, 4 * W, W), A("kt"), 0.0, NE, D, MAX)
+    ts(A("in1"), A("mk"), 228.0, ADD, -1.0 / 1024, MUL)
+    step_row(1, cp)
 
     for t in range(R):
-        last = t == R - 1
+        first, last = t == 0, t == R - 1
         to = T.cores[(rank + STEP[t]) % n]
         frm = T.cores[(rank - STEP[t]) % n]
         qt, st = A("qt", C * t, C * t + C), A("st", C * t, C * t + C)
-        x0, l0 = XW * t, 16 * t
+        l0 = 16 * t
         mm(bank(0), A("qab", 0, 128), A("sab", 0, 128), qt, st)
         mm(bank(1), A("qab", 128, 256), A("sab", 128, 256), qt, st)
-        if t == 0:
-            marks(0)
+        act(A("ya"), bank(0), AF.Sign, scale=col(SGA), bias=col(EPA))
+        act(A("yb"), bank(1), AF.Sign, scale=col(SGB), bias=col(EPB))
+        if first:
+            step_row(3, act)
+        scan(A("z1"), A("place"), A("ya"), -1.0, MAX, MIN)
+        if first:
             unit(0)
-        else:
-            pad(t)
-        ts(A("ay", 0, C), bank(0), 0.0, LT, lacol, EQ)
-        act(A("ay", C, 2 * C), bank(1), AF.Sign, scale=col(SIG), bias=col(EPS))
-        if t == 0:
-            step_row(2)
-            step_row(3)
+        tt(A("xv", 1, C + 1), A("z1"), A("yb"), MIN)
+        if first:
             unit(1)
-        else:
-            scan(A("day", 0, C), A("cd"), A("ay", 0, C), 0.0)
-        tt(A("xr", x0, x0 + C), A("ay", 0, C), A("ay", C, 2 * C), MUL)
+
+        def own():
+            for b, k in ((0, 2), (1, 3), (2, 6), (3, 7)):
+                unpack(k, b, qt, st)
+            for b in range(2):
+                act(A("fo", C * b, C * b + C), bank(2 + b))
+
+        if not first:
+            own()
         for s in range(4):
-            scan(A("so1", W * s, W * s + 226 + s), A("cb", W * s, W * s + 226 + s), A("xr", x0, x0 + 226 + s), A("ini", s, s + 1))
-        fin1 = A("so1", 225, 4 * W, W + 1)
+            scan(A("so1", W * s, W * s + N1), A("cb", W * s, W * s + N1), A("xv", 0, N1), A("in1", s, s + 1))
+        fin1 = A("so1", N1 - 1, 4 * W, W)
         f16 = A("lst", l0, l0 + 4)
-        ts(f16, fin1, -512.0, MUL, 223.0, ADD)
-        act(A("xr", x0 + 225, x0 + 229), fin1, AF.Identity, bias=-0.5)
-        cp(IND(A("xr", x0, x0 + 293), f16), A("zero", 0, 64))
-        act(A("frv"), IND(A("tv", 0, 293), f16))
+
+        def behind(s):
+            ts(A("d2", W * s + 1, W * s + 1 + C), A("xv", 1, C + 1), A("so1", W * s + N1 - 1, W * s + N1), ADD, 126.5 / 1024, GT)
+
+        behind(0)
+        behind(1)
+        ts(f16, fin1, -1024.0, MUL, 126.0, ADD)
+        ts(A("in2"), fin1, 2.0, MUL, 160.0 / 512, ADD)
+        behind(2)
+        behind(3)
+        act(A("frv"), IND(A("tv"), f16))
         for s in range(4):
-            act(A("junk", 64 * s, 64 * s + 64), A("frv"), AF.Sign, acc=A("acc", s, s + 1), scale=-D,
-                bias=A("so1", (W + 1) * s + 225, (W + 1) * s + 226))
+            act(A("junk", 64 * s, 64 * s + 64), A("frv"), AF.Sign, acc=A("acc", s, s + 1), scale=1.0 / 1024,
+                bias=A("so1", W * s + N1 - 1, W * s + N1))
         for s in range(4):
-            scan(A("so2", W * s, W * s + 226 + s), A("cb", W * s, W * s + 226 + s), A("xr", x0, x0 + 226 + s), A("ini", s, s + 1))
-        ts(A("lst", l0 + 4, l0 + 8), A("so2", 225, 4 * W, W + 1), -512.0, MUL, 223.0, ADD)
+            scan(A("so2", W * s, W * s + N2), A("cb", W * s, W * s + N2), A("d2", W * s, W * s + N2), A("in2", s, s + 1))
+        if first:
+            ts(A("io"), A("tv", 0, 64), 126.0, ADD)
+            unit(2)
+        else:
+            hold(A("da"), A("ya"), A("cda", 0, C))
+        ts(A("lst", l0 + 4, l0 + 8), A("so2", N2 - 1, 4 * W, W), -512.0, MUL, 255.0, ADD)
         send(to, A("ll", l0, l0 + 8), A("lst", l0, l0 + 8), "larr%d" % t)
-        ts(A("r16"), A("acc"), -0.5, MUL, 31.5, ADD)
+        ts(A("r16"), A("acc"), 0.5, MUL, 31.5, ADD) if False else ts(A("r16"), A("acc"), -0.5, MUL, 31.5, ADD)
+
+        def key_b():
+            ts(A("cdb", 15, C, 16), A("da", 15, C, 16), col(B0), MUL, col(B1), ADD)
+
+        def key_list():
+            ts(A("k16", 0, 14), A("db", 15, C, 16), col(K0), MUL, col(K1), ADD)
+
+        if first:
+            unit(3)
+        else:
+            key_b()
         cp(IND(A("srt"), A("r16")), A("io"))
-        scan(A("sol"), A("cd", 0, 64), A("srt"), 0.0)
-        ts(A("lst", l0 + 8, l0 + 12), A("sol", 15, 64, 16), col(LAM), SUB)
+        if first:
+            ts(col(A0), col(SGA), -4.0, MUL)
+            ts(col(A1), col(SGA), -256.0, MUL, end, ADD)
+            ts(col(B0), col(SGA), 2.0, MUL, col(SGB), MUL)
+        else:
+            hold(A("db"), A("yb"), A("cdb", 0, C))
+        hold(A("sol"), A("srt"), A("cd", 0, 64))
+        if first:
+            cp(A("cda"), A("cd"))
+            cp(A("cdb"), A("cd"))
+        else:
+            cp(A("r4"), IND(A("m4"), A("r16"))) if not last else None
+        ts(A("lst", l0 + 8, l0 + 12), A("sol", 15, 64, 16), 64.0, ADD)
         send(to, A("ll", l0 + 8, l0 + 12), A("lst", l0 + 8, l0 + 12), "karr%d" % t)
+        if not first:
+            key_list()
         lq, ls = A("lq", C * t, C * t + C), A("ls", C * t, C * t + C)
         arrive(frm, 2, "qarr%d" % t, [lq, ls])
-        if t == 0:
-            unit(2)
-            unit(3)
-        act(A("rk"), IND(A("io"), A("r16")))
+        fb = (4, 5, 0, 1)
         for b in range(4):
-            unpack(4 + b, b, lq, ls)
-        for b in (0, 2):
-            act(A("fh", FW * b, FW * b + C), bank(4 + b), AF.Identity, scale=0.5)
-        act(A("fh", FW * 2 + 256, FW * 2 + 256 + C), bank(6), AF.Identity, scale=0.5)
+            unpack(fb[b], b, lq, ls)
+        if first:
+            own()
 
-        def half(b):
-            ts(A("fh", FW * b, FW * b + C), bank(4 + b), 0.5, MUL)
+        def half_s(b, a):
+            act(A("fh", FW * b + a, FW * b + a + C), bank(fb[b]), AF.Identity, scale=0.5)
+
+        def half_v(b):
+            ts(A("fh", FW * b, FW * b + C), bank(fb[b]), 0.5, MUL)
 
         def again(b):
-            cp(A("fh", FW * b + 256, FW * b + 256 + C), A("fh", FW * b, FW * b + C))
+            cp(A("fh", FW * b + C, FW * b + 2 * C), A("fh", FW * b, FW * b + C))
 
-        if t == 0:
-            ts(col(AA), lacol, 4.0, MUL, -2.0, ADD)
-            ts(col(AY), col(SIG), -0.5, MUL)
-            ts(col(BP), lacol, -2.0, MUL, 2.5, ADD)
-            scan(A("day", 0, C), A("cd"), A("ay", 0, C), 0.0)
-            ts(col(TMP), col(AA), col(AY), ADD, col(LAM), MUL)
-        scan(A("day", C, 2 * C), A("cd"), A("ay", C, 2 * C), 0.0)
-        if t == 0:
-            ts(col(BETA), col(BP), col(TMP), SUB)
-        ts(A("t2", 0, 14), A("day", C + 15, 2 * C, 16), col(AY), MUL)
-        ts(A("t1", 0, 14), A("day", 15, C, 16), col(AA), MUL, col(BETA), ADD)
-        tt(A("t3", 0, 14), A("t2", 0, 14), A("h4", 0, 14), ADD)
-        half(1)
+        if first:
+            ops.extend([ops.pop(-2), ops.pop(-1)][::1]) if False else None
+        half_s(0, 0)
+        half_s(2, 0)
+        half_s(2, C)
+        if first:
+            key_steps()
+            ts(col(B1), col(B0), 64.0, MUL, end, ADD)
+        half_v(1)
         again(0)
-        tt(A("t4", 0, 14), A("t3", 0, 14), A("t1", 0, 14), ADD)
-        half(3)
+        half_v(3)
         again(1)
-        cp(A("k16", 0, 14), A("t4", 0, 14))
+        if first:
+            hold(A("da"), A("ya"), A("cda", 0, C))
         again(3)
+        act(A("rk"), IND(A("io"), A("r16")))
         arrive(frm, 1, "larr%d" % t, [A("ll", l0, l0 + 8)])
         arrive(frm, 1, "karr%d" % t, [A("ll", l0 + 8, l0 + 12)])
+        if first:
+            ts(col(B1), col(B1), -64.0, ADD)
+            ts(col(K0), col(SGB), -0.5, MUL)
+            ts(col(K1), col(SGB), -64.0, MUL, 1.5, ADD)
+            act(A("zt", 256, 512), A("zero", 0, 256))
         sec = [IND(A("fh", FW * b, FW * b + FW), A("ll", l0 + 4, l0 + 8)) for b in range(4)]
         cp(A("zs", 0, 64), sec[0])
         for b in range(1, 4):
             act(A("zs", 64 * b, 64 * b + 64), sec[b])
         for b in range(4):
-            tt(A("zk", 64 * b, 64 * b + 64), IND(A("fh", FW * b + 256, FW * b + FW), A("ll", l0, l0 + 4)), A("zs", 64 * b, 64 * b + 64), ADD)
+            tt(A("zk", 64 * b, 64 * b + 64), IND(A("fh", FW * b + C, FW * b + FW), A("ll", l0, l0 + 4)), A("zs", 64 * b, 64 * b + 64), ADD)
         for b in range(4):
             (act if b < 2 else cp)(A("zt", b, 256, 4), IND(A("zk", 64 * b, 64 * b + 64), A("ll", l0 + 8, l0 + 12)))
         quant(A("qz"), A("sz"), A("zt"))
         for b in range(4):
             mm(bank(b, 0, 128), A("wq", 128 * b, 128 * b + 128), A("wsc", 128 * b, 128 * b + 128), A("qz"), A("sz"))
-        if last:
-            quant(A("qv"), A("sv"), A("vt"))
-        else:
-            cp(A("r4"), IND(A("m4"), A("r16")))
-            marks(t + 1)
-        for b in range(4):
-            if b % 2 == 0:
-                act(A("ht", b, 256, 4), bank(b, 0, 64), AF.Relu, scale=0.03125)
-            else:
-                ts(A("ht", b, 256, 4), bank(b, 0, 64), 0.0, MAX, 0.03125, MUL)
-        h0, h1 = 128 * t, 192 * t
-        quant(A("qh", h0, h0 + 128), A("sh", h0, h0 + 128), A("ht"))
-        send(frm, u8("hq", h1 + 128, h1 + 192), u8("qh", h0, h0 + 64), "harr%d" % t)
-        send(frm, A("hs", h1 + 128, h1 + 192), A("sh", h0, h0 + 64), "harr%d" % t)
-        for b in range(4):
-            unpack(4 + b, b, qt, st)
         cr = A("crf") if last else A("crow")
-        act(cr, IND(A("rk"), A("k16", 0, 14)))
-        for b in range(2):
-            act(A("fo", C * b, C * b + C), bank(4 + b))
-        if t == 0:
-            pad(0)
-        if not last:
+
+        def class_row():
+            act(cr, IND(A("rk"), A("k16", 0, 14)))
+
+        def low_rows():
             cp(A("cm4"), IND(A("r4"), A("k16", 0, 14)))
-        scan(A("dc"), A("cd"), cr, 0.0)
-        if not last:
-            high_a()
-        ts(A("c16", 0, 14), A("dc", 15, C, 16), col(LAM), SUB)
-        if not last:
-            high_b()
-            high_c()
-            step_row(0)
-            step_row(1)
-        arrive(to, 2, "harr%d" % t, [A("hq", h1 + 128, h1 + 192), A("hs", h1 + 128, h1 + 192)])
+
+        def class_hold():
+            hold(A("dc"), cr, A("cd", 0, C))
+
+        def own_part():
+            ts(A("cm16"), A("cm4"), 4.0, MUL)
+
+        def class_list():
+            ts(A("c16", 0, 14), A("dc", 15, C, 16), 64.0, ADD)
+
+        if first:
+            act(A("ht", 256, 512), A("zero", 0, 256))
+            key_b()
+            cp(A("r4"), IND(A("m4"), A("r16")))
+            hold(A("db"), A("yb"), A("cdb", 0, C))
+            quant(A("hq", 0, 128), A("hs", 0, 128), A("zero"))
+            key_list()
+        else:
+            class_row()
+            if last:
+                quant(A("qv"), A("sv"), A("vt"))
+                class_hold()
+            else:
+                low_rows()
+                class_hold()
+                own_part()
+            class_list()
         for b in range(4):
-            unpack(b, b, A("hq", h1 + 64, h1 + 192), A("hs", h1 + 64, h1 + 192), 128)
-        for b in range(4):
-            (cp if b < 2 else act)(A("gd", 64 * b, 64 * b + 64), bank(b, 64, 128))
-        if t == 0:
+            act(A("ht", b, 256, 4), bank(b, 0, 64), AF.Relu, scale=0.03125)
+        h0, h1 = 128 * t, 128 + K * t
+        quant(A("qh", h0, h0 + 128), A("sh", h0, h0 + 128), A("ht"))
+        send(frm, u8("hq", h1, h1 + K), u8("qh", h0, h0 + K), "harr%d" % t)
+        send(frm, A("hs", h1, h1 + K), A("sh", h0, h0 + K), "harr%d" % t)
+        if first:
+            class_row()
+            low_rows()
+            class_hold()
+            own_part()
+            class_list()
+        if not last:
+            high_row()
+            high_hold()
+            high_steps()
+            key_steps()
+            pair_hold()
+            pair_list()
+        arrive(to, 2, "harr%d" % t, [A("hq", h1, h1 + K), A("hs", h1, h1 + K)])
+        hb_ = (4, 5, 2, 3)
+        for b in (2, 0, 3, 1):
+            unpack(hb_[b], b, A("hq", h1 - K, h1 + K), A("hs", h1 - K, h1 + K), 128)
+        for b in (2, 0, 3, 1):
+            (cp if b < 2 else act)(A("gd", 64 * b, 64 * b + 64), bank(hb_[b], 64, 128))
+        if first:
             dma("Y", "v", lambda: T["vt"][:], lambda: T.v[:], [A("vt")], [A("gd", 0, 64)])
         if last:
             dma("Y", "ol", lambda: T.ol[:], lambda: T["crf"][0:128:16, :], [], [cr, A("c16", 0, 14)])
@@ -424,8 +499,10 @@ def rank_program(g, core, T, topo):
         quant(A("qt", C * t + C, C * t + 2 * C), A("st", C * t + C, C * t + 2 * C), A("tn"))
         if not last:
             send_state(t + 1)
-            step_row(2)
-            step_row(3)
+            step_row(2, act)
+            step_row(3, act)
+            step_row(0, cp)
+            step_row(1, cp)
 
     q0 = R * C
     mm(bank(0, 0, 128), A("qv"), A("sv"), A("qt", q0, q0 + 128), A("st", q0, q0 + 128))

@@ -4,6 +4,7 @@ from concourse.mybir import dt, AluOpType, ActivationFunctionType
 
 C, K, R = 224, 64, 3
 STEP = [1, 2, 4]
+P = 256
 W = 244
 N1, N2 = 227, 228
 FW = 512
@@ -17,30 +18,29 @@ def _sb(n, t):
 
 
 SCRATCH = {
-    "xt": _sb(896, BF), "ut": _sb(512, BF), "vt": _sb(512, BF), "nx32": _sb(16, I32), "co32": _sb(16, I32),
+    "xt": _sb(4 * P, BF), "ut": _sb(512, BF), "vt": _sb(512, BF), "nx32": _sb(16, I32), "co32": _sb(16, I32),
     "wq": _sb(512, MX), "wsc": _sb(512, U8),
     "qu": _sb(128, MX), "su": _sb(128, U8), "qab": _sb(256, MX), "sab": _sb(256, U8),
     "qv": _sb(128, MX), "sv": _sb(128, U8), "qe": _sb(512, MX), "se": _sb(512, U8),
-    "qt": _sb(4 * C, MX), "st": _sb(4 * C, U8), "lq": _sb(3 * C, MX), "ls": _sb(3 * C, U8),
+    "qt": _sb(4 * P, MX), "st": _sb(4 * P, U8), "lq": _sb(3 * C, MX), "ls": _sb(3 * C, U8),
     "qz": _sb(128, MX), "sz": _sb(128, U8), "qh": _sb(3 * 128, MX), "sh": _sb(3 * 128, U8),
     "hq": _sb(128 + 3 * K, MX), "hs": _sb(128 + 3 * K, U8),
-    "tn": _sb(896, BF), "zt": _sb(512, BF), "ht": _sb(512, BF), "zero": _sb(512, BF), "eb": _sb(520, BF), "ones": _sb(288, BF),
+    "tn": _sb(4 * P, BF), "zt": _sb(512, BF), "ht": _sb(512, BF), "zero": _sb(512, BF), "eb": _sb(520, BF), "ones": _sb(128, BF),
     "fh": _sb(4 * FW, BF), "fo": _sb(448, BF), "gd": _sb(256, BF), "zs": _sb(256, BF), "zk": _sb(256, BF), "ge": _sb(448, BF),
     "yo": _sb(C, F32),
     "lst": _sb(3 * 16, U16), "ll": _sb(3 * 16, U16), "nx16": _sb(16, U16), "co16": _sb(16, U16), "c16": _sb(16, U16),
     "k16": _sb(16, U16), "p16": _sb(16, U16), "r16": _sb(4, U16), "u16": _sb(16, U16), "cd16": _sb(16, U16), "ct16": _sb(72, U16),
-    "ya": _sb(C, BF), "yb": _sb(C, BF), "z1": _sb(C, BF), "xv": _sb(W, BF), "cb": _sb(4 * W, BF), "so1": _sb(4 * W, BF),
+    "ya": _sb(C, BF), "yb": _sb(C, BF), "xr": _sb(W, BF), "xv": _sb(W, BF), "cb": _sb(4 * W, BF), "so1": _sb(4 * W, BF),
     "d2": _sb(4 * W, BF), "so2": _sb(4 * W, BF), "in1": _sb(4, F32), "in2": _sb(4, F32),
     "frv": _sb(64, BF), "junk": _sb(256, BF), "acc": _sb(4, F32), "srt": _sb(64, BF), "sol": _sb(64, BF),
     "da": _sb(C, BF), "db": _sb(C, BF), "rk": _sb(64, BF), "r4": _sb(64, BF), "crow": _sb(C, BF), "crf": _sb(C, F32), "dc": _sb(C, BF),
     "cm4": _sb(C, BF), "cm16": _sb(C, BF), "hb": _sb(W, BF), "dh": _sb(240, BF), "dp": _sb(240, BF),
     "cdp": _sb(240, BF), "cda": _sb(240, BF), "cdb": _sb(240, BF),
-    "pi": _sb(1, I32), "ci": _sb(4, I32), "cf": _sb(4, F32), "col": _sb(16, F32), "r16f": _sb(16, F32), "kt": _sb(4, F32),
-    "mk": _sb(4, F32), "w1": _sb(72, F32), "w2": _sb(72, F32), "w3": _sb(72, F32), "w4": _sb(72, F32), "w5": _sb(72, F32),
-    "w6": _sb(72, F32), "w7": _sb(72, F32), "a36": _sb(36, F32), "b36": _sb(36, F32), "n36": _sb(72, F32), "d36": _sb(36, F32),
-    "t36": _sb(36, BF), "ctab": _sb(1152, BF), "e0": _sb(16, F32), "e1": _sb(16, F32), "e2": _sb(16, F32), "e3": _sb(16, F32),
-    "wr": _sb(16, F32), "cds": _sb(16, BF), "cd": _sb(240, BF), "m4": _sb(64, BF), "io": _sb(64, BF), "tv": _sb(288, BF),
-    "place": _sb(C, BF),
+    "pi": _sb(1, I32), "ci": _sb(4, I32), "cf": _sb(4, F32), "col": _sb(16, F32), "kt": _sb(4, F32), "u32": _sb(16, I32),
+    "c4": _sb(4, F32), "w1": _sb(72, F32), "w3": _sb(72, F32), "w5": _sb(4, F32), "w6": _sb(4, F32),
+    "a36": _sb(36, F32), "b36": _sb(36, F32), "n36": _sb(72, F32), "t36": _sb(36, BF), "ctab": _sb(1152, BF),
+    "e0": _sb(16, F32), "e1": _sb(16, F32), "wr": _sb(16, F32), "cds": _sb(16, BF), "cd": _sb(240, BF),
+    "m4": _sb(64, BF), "io": _sb(64, BF), "tv": _sb(288, BF), "place": _sb(C, BF),
     "ps": ("psum", [128, 4096], F32),
 }
 LOADS = ["co", "nx", "x", "u", "wc", "ws", "v"]
@@ -101,8 +101,7 @@ def rank_program(g, core, T, topo):
                 wr += _cells(v)
         for v in ins:
             if isinstance(v, tuple):
-                for c in _cells(v):
-                    (wr if c[0] == "ps" else rd).append(c)
+                rd += _cells(v)
         ops.append({"q": q, "call": call, "wr": wr, "rd": rd, "sem": sem, "val": val})
 
     def ts(out, a, s1, op0, s2=None, op1=None):
@@ -137,6 +136,12 @@ def rank_program(g, core, T, topo):
             return g.scalar.activation(real(out), real(a), f, **k)
         op("S", call, [out] + ([] if acc is None else [acc]), [a] + list(kw.values()))
 
+    def lin(out, a, scale, bias):
+        act(out, a, AF.Identity, scale=scale, bias=bias)
+
+    def sfill(out, c):
+        lin(out, A("zero", 0, len(range(out[2], out[3], out[4]))), 1.0, c)
+
     def mm(out, wq, wsc, q, s):
         op("P", lambda: g.tensor.matmul_mx(real(out), real(wq), real(wsc), real(q), real(s), True, True), [out], [wq, wsc, q, s])
 
@@ -167,79 +172,33 @@ def rank_program(g, core, T, topo):
     def u8(name, a, b):
         return A(name, a, b, 1, dt.uint8)
 
+    def u32(name, a, b):
+        return A(name, a, b, 1, dt.uint32)
+
     def col(k):
         return A("col", k, k + 1)
 
-    SGA, SGB, EPA, EPB, Q1, PC, A0, A1, B0, B1, K0, K1 = range(12)
+    SGA, SGB, EPA, EPB, TMP, PC, A0, A1, B0, B1, B2, K0, K1 = range(13)
     icol, qcol, lacol, lbcol = [A("cf", k, k + 1) for k in range(4)]
     end = A("cds", 15, 16)
 
-    dma("Y", "co", lambda: T["co32"][:, 0:14], lambda: T.co[:], [A("co32", 0, 14)], [])
-    dma("S", "x", lambda: T["xt"][:], lambda: T.x[:], [A("xt")], [])
-    dma("Y", "nx", lambda: T["nx32"][:, 0:14], lambda: T.nx[:], [A("nx32", 0, 14)], [])
-    dma("Y", "u", lambda: T["ut"][:], lambda: T.u[:], [A("ut")], [])
-    dma("Y", "wc", lambda: T["wq"][:].bitcast(dt.uint8), lambda: T.wc[:], [A("wq")], [A("nx32", 0, 14)])
-    dma("Y", "ws", lambda: T["wsc"][:], lambda: T.ws[:], [A("wsc")], [])
+    def half(t, a):
+        return A("qt", P * t + a, P * t + a + 128), A("st", P * t + a, P * t + a + 128)
 
-    iota(A("pi"), [[1, 1]], 0, 1)
-    iota(A("w2"), [[-4, 4], [0, 18]])
-    iota(A("w1"), [[-4, 4], [1, 18]])
-    iota(A("a36"), [[1, 6], [0, 6]])
-    iota(A("b36"), [[0, 6], [1, 6]])
-    iota(A("m4"), [[0, 16], [1, 4]])
-    fill(A("ones"), 1.0)
-    fill(A("eb"), 0.0)
-    fill(A("xv"), -1.0)
-    fill(A("hb"), 0.0)
-    scan(A("tv"), A("ones"), A("ones"), -127.0, ADD, MUL)
-    ts(A("ci", 0, 1), A("pi"), 15, AND)
-    ts(A("ci", 1, 2), A("pi"), 2, SHR, 3, AND)
-    ts(A("ci", 2, 3), A("pi"), 1, SHR, 1, AND)
-    ts(A("ci", 3, 4), A("pi"), 1, AND)
-    ts(A("r16f"), A("tv", 0, 16), 126.0, ADD)
-    fill(A("hb", 225, 227), 16.0)
-    cp(A("cf"), A("ci"))
-    act(A("zero"), A("eb", 0, 512))
-    for b in range(4):
-        act(A("fh", FW * b + 2 * C, FW * b + FW), A("eb", 0, 64))
-    act(A("d2", 0, 4 * W, W), A("eb", 0, 4), AF.Identity, bias=-2.0)
-    for k in range(225, 228):
-        act(A("d2", k, 4 * W, W), A("eb", 0, 4), AF.Identity, bias=-2.0)
-    ts(A("w3"), A("w1"), -1.0, MAX, 4.0, MIN)
-    fill(A("hb", 227, 228), 16.25)
-    ts(A("w5"), A("w2"), icol, ADD, -1.0, MAX)
-    ts(col(Q1), qcol, 1.0, ADD)
-    ts(A("w4"), A("w3"), 6.0, MUL, 7.0, ADD)
-    ts(A("wr"), A("r16f"), icol, SUB)
-    ts(A("w6"), A("w5"), 4.0, MIN)
-    ts(A("n36", 0, 36), A("a36"), col(Q1), NE)
-    ts(A("n36", 36, 72), A("b36"), col(Q1), NE)
-    ts(A("e0"), A("wr"), -1.0, EQ, -256.0, MUL)
-    tt(A("w7"), A("w4"), A("w6"), ADD)
-    ts(A("e1"), A("wr"), 0.0, EQ, 64.0, MUL)
-    tt(A("d36"), A("n36", 0, 36), A("n36", 36, 72), SUB)
-    ts(A("e2"), A("r16f"), 15.0, EQ, -128.0, MUL)
-    cp(A("ct16"), A("w7"))
-    tt(A("e3"), A("e0"), A("e1"), ADD)
-    ts(A("t36"), A("d36"), L, MUL, D, ADD)
-    ts(A("cd16"), A("r16f"), 0.0, MUL, icol, ADD)
-    ts(col(SGA), lacol, -2.0, MUL, 1.0, ADD)
-    tt(A("cds"), A("e3"), A("e2"), ADD)
-    act(A("ctab", 0, 576), IND(A("t36"), A("ct16", 0, 36)))
-    act(A("ctab", 576, 1152), IND(A("t36"), A("ct16", 36, 72)))
-    op("G", lambda: g.affine_select(T["eb"][:, 3:515:4], T["ones"][:, 0:128], [[1, 128]], EQ, 0.0, 0, -1),
-       [A("eb", 3, 515, 4)], [A("ones", 0, 128)])
-    ts(A("u16", 0, 8), A("r16f", 0, 8), 16.0, MUL)
-    ts(A("u16", 8, 16), A("r16f", 0, 8), 16.0, MUL, 1.0, ADD)
-    cp(A("cd"), IND(A("cds"), A("cd16", 0, 15)))
+    def state(t, tile):
+        for a in (0, 128):
+            quant(*half(t, a), A(tile, 4 * a, 4 * a + 512))
 
     def send_state(t):
         to = T.cores[(rank + STEP[t]) % n]
-        send(to, u8("lq", C * t, C * t + C), u8("qt", C * t, C * t + C), "qarr%d" % t)
-        send(to, A("ls", C * t, C * t + C), A("st", C * t, C * t + C), "qarr%d" % t)
+        send(to, u8("lq", C * t, C * t + C), u8("qt", P * t, P * t + C), "qarr%d" % t)
+        send(to, A("ls", C * t, C * t + C), A("st", P * t, P * t + C), "qarr%d" % t)
 
     def step_row(s, on):
         on(A("cb", W * s + 1, W * s + 241), IND(A("ctab", 288 * s, 288 * s + 288), A("p16", 0, 15)))
+
+    def own_part():
+        ts(A("cm16"), A("cm4"), 4.0, MUL)
 
     def high_row():
         tt(A("hb", 1, C + 1), IND(A("cm4"), A("nx16", 0, 14)), A("cm16"), ADD)
@@ -250,66 +209,129 @@ def rank_program(g, core, T, topo):
     def high_steps():
         ts(A("cdp", 15, 240, 16), A("dh", 15, 240, 16), 16.0, MUL, col(PC), ADD)
 
-    def key_steps():
-        ts(A("cda", 15, C, 16), A("dh", 15, C, 16), col(A0), MUL, col(A1), ADD)
-
     def pair_hold():
         hold(A("dp"), A("hb", 0, 240), A("cdp"))
 
     def pair_list():
         ts(A("p16", 0, 15), A("dp", 15, 240, 16), 256.0, ADD)
 
+    def key_steps():
+        ts(A("cda", 15, C, 16), A("dh", 15, C, 16), col(A0), MUL, col(A1), ADD)
+
+    def key_a():
+        hold(A("da"), A("ya"), A("cda", 0, C))
+
+    def key_steps_b():
+        ts(A("cdb", 15, C, 16), A("da", 15, C, 16), col(B0), MUL, col(B1), ADD)
+
+    def key_b():
+        hold(A("db"), A("yb"), A("cdb", 0, C))
+
+    def key_list():
+        ts(A("k16", 0, 14), A("db", 15, C, 16), col(K0), MUL, col(K1), ADD)
+
+    def low_keys():
+        cp(A("r4"), IND(A("m4"), A("r16")))
+
+    def low_row():
+        cp(A("cm4"), IND(A("r4"), A("k16", 0, 14)))
+
+    def class_list():
+        ts(A("c16", 0, 14), A("dc", 15, C, 16), 64.0, ADD)
+
     def unit(b):
         quant(A("qe", 128 * b, 128 * b + 128), A("se", 128 * b, 128 * b + 128), A("eb", 3 - b, 515 - b))
 
+    dma("Y", "co", lambda: T["co32"][:, 0:14], lambda: T.co[:], [A("co32", 0, 14)], [])
+    dma("S", "x", lambda: T["xt"][:, 0:4 * C], lambda: T.x[:], [A("xt", 0, 4 * C)], [])
+    dma("Y", "nx", lambda: T["nx32"][:, 0:14], lambda: T.nx[:], [A("nx32", 0, 14)], [])
+    dma("Y", "u", lambda: T["ut"][:], lambda: T.u[:], [A("ut")], [])
+    dma("Y", "wc", lambda: T["wq"][:].bitcast(dt.uint8), lambda: T.wc[:], [A("wq")], [A("ut")])
+    dma("Y", "ws", lambda: T["wsc"][:], lambda: T.ws[:], [A("wsc")], [])
+
+    iota(A("pi"), [[1, 1]], 0, 1)
+    iota(A("c4"), [[-4, 4]])
+    iota(A("a36"), [[1, 6], [0, 6]], -1)
+    iota(A("b36"), [[0, 6], [1, 6]], -1)
+    iota(A("w1"), [[-4, 4], [1, 18]])
+    iota(A("io"), [[1, 64]])
+    iota(A("m4"), [[0, 16], [1, 4]])
+    iota(A("u32"), [[1, 2], [16, 8]])
+    iota(A("tv"), [[1, 288]], -159)
+    fill(A("zero"), 0.0)
+    fill(A("hb"), 0.0)
+    ts(A("ci", 0, 1), A("pi"), 15, AND)
+    ts(A("ci", 1, 2), A("pi"), 2, SHR, 3, AND)
+    ts(A("ci", 2, 3), A("pi"), 1, SHR, 1, AND)
+    ts(A("ci", 3, 4), A("pi"), 1, AND)
+    fill(A("eb"), 0.0)
+    cp(A("cf"), A("ci"))
+    fill(A("xr"), -1.0)
+    fill(A("e0", 15, 16), -128.0)
+    sfill(A("xt", 4 * C, 4 * P), 0.0)
+    sfill(A("hb", 225, 227), 16.0)
+    sfill(A("hb", 227, 228), 16.25)
+    sfill(A("ones"), 1.0)
+    sfill(A("xv", 0, W, C + 1), -1.0)
+    sfill(A("d2", N2 - 1, 4 * W, W), -2.0)
+    sfill(A("d2", N2 - 2, 4 * W, W), -2.0)
+    ts(A("w5"), A("c4"), icol, ADD, -1.0, MAX)
+    ts(A("n36", 0, 36), A("a36"), qcol, NE, D, MAX)
+    ts(A("n36", 36, 72), A("b36"), qcol, NE, L, MUL)
+    ts(A("w3"), A("w1"), -1.0, MAX, 4.0, MIN)
+    ts(A("w6"), A("w5"), 4.0, MIN, 7.0, ADD)
+    ts(A("wr"), A("io", 0, 16), icol, SUB)
+    tt(A("t36"), A("n36", 0, 36), A("n36", 36, 72), SUB)
+    ts(A("cd16"), A("io", 0, 16), 0.0, MUL, icol, ADD)
+    for s in range(4):
+        ts(A("ct16", 18 * s, 18 * s + 18), A("w3", 18 * s, 18 * s + 18), 6.0, MUL, A("w6", s, s + 1), ADD)
+    ts(A("e0", 0, 15), A("wr", 0, 15), -1.0, EQ, -256.0, MUL)
+    ts(A("e1"), A("wr"), 0.0, EQ, 64.0, MUL)
+    lin(col(SGA), lacol, -2.0, 1.0)
+    lin(col(SGB), lbcol, -2.0, 1.0)
+    lin(col(TMP), icol, -D, 286.0 * D)
+    lin(col(EPA), col(SGA), 2.0 ** -120, 0.0)
+    lin(col(EPB), col(SGB), 2.0 ** -120, 0.0)
+    lin(A("kt"), A("m4", 0, 4), 4.0, qcol)
+    lin(A("in1"), A("m4", 0, 4), -16.0 * D, col(TMP))
+    act(A("ctab", 0, 576), IND(A("t36"), A("ct16", 0, 36)))
+    act(A("ctab", 576, 1152), IND(A("t36"), A("ct16", 36, 72)))
+
     cp(A("co16", 0, 14), A("co32", 0, 14))
     cp(A("nx16", 0, 14), A("nx32", 0, 14))
-    ts(col(PC), end, 832.0, ADD)
+    tt(A("cds"), A("e0"), A("e1"), ADD)
+    cp(A("u16"), A("u32"))
     cp(A("cm4"), IND(A("m4"), A("co16", 0, 14)))
-    quant(A("qt", 0, C), A("st", 0, C), A("xt"))
-    ts(A("cm16"), A("cm4"), 4.0, MUL)
+    cp(A("cd"), IND(A("cds"), A("cd16", 0, 15)))
+    own_part()
+    state(0, "xt")
     send_state(0)
-    quant(A("qu"), A("su"), A("ut"))
+    op("G", lambda: g.affine_select(T["eb"][:, 3:515:4], T["ones"][:], [[1, 128]], EQ, 0.0, 0, -1), [A("eb", 3, 515, 4)], [A("ones")])
     high_row()
-    act(A("sab"), IND(A("su"), A("u16")))
+    quant(A("qu"), A("su"), A("ut"))
+    lin(col(PC), end, 1.0, 832.0)
     cp(A("cdp"), A("cd"))
     high_hold()
-    ts(col(SGB), lbcol, -2.0, MUL, 1.0, ADD)
-    ts(col(EPA), col(SGA), 2.0 ** -120, MUL)
+    act(A("sab", 0, 128), IND(A("su"), A("u16", 0, 8)))
+    act(A("sab", 128, 256), IND(A("su"), A("u16", 8, 16)))
+    sfill(A("ctab", 272, 1152, 288), -2.125)
+    sfill(A("ctab", 276, 1152, 288), 0.1875)
+    lin(A("place"), A("tv", 0, C), D, 159.0 * D)
+    cp(u32("qab", 0, 128), IND(u32("qu", 0, 128), A("u16", 0, 8)))
     high_steps()
-    cp(A("qab", 0, 256, 1, dt.uint32), IND(A("qu", 0, 128, 1, dt.uint32), A("u16")))
+    cp(u32("qab", 128, 256), IND(u32("qu", 0, 128), A("u16", 8, 16)))
     pair_hold()
-    ts(col(EPB), col(SGB), 2.0 ** -120, MUL)
-    fill(A("ctab", 272, 1152, 288), -1.3125)
-    fill(A("ctab", 276, 1152, 288), -0.625)
-    pair_list()
-    ts(A("place"), A("tv", 0, C), 126.0, ADD, 1.0 / 1024, MUL)
-    ts(A("kt"), A("r16f", 0, 4), 4.0, MUL, qcol, ADD)
-    ts(A("mk"), A("r16f", 0, 4), 16.0, MUL, icol, ADD)
-    step_row(0, cp)
-    step_row(2, act)
     ts(A("cb", 0, 4 * W, W), A("kt"), 0.0, NE, D, MAX)
-    ts(A("in1"), A("mk"), 228.0, ADD, -1.0 / 1024, MUL)
-    step_row(1, cp)
+    cp(A("cda"), A("cd"))
+    pair_list()
 
     for t in range(R):
         first, last = t == 0, t == R - 1
         to = T.cores[(rank + STEP[t]) % n]
         frm = T.cores[(rank - STEP[t]) % n]
-        qt, st = A("qt", C * t, C * t + C), A("st", C * t, C * t + C)
+        qt, st = A("qt", P * t, P * t + C), A("st", P * t, P * t + C)
         l0 = 16 * t
-        mm(bank(0), A("qab", 0, 128), A("sab", 0, 128), qt, st)
-        mm(bank(1), A("qab", 128, 256), A("sab", 128, 256), qt, st)
-        act(A("ya"), bank(0), AF.Sign, scale=col(SGA), bias=col(EPA))
-        act(A("yb"), bank(1), AF.Sign, scale=col(SGB), bias=col(EPB))
-        if first:
-            step_row(3, act)
-        scan(A("z1"), A("place"), A("ya"), -1.0, MAX, MIN)
-        if first:
-            unit(0)
-        tt(A("xv", 1, C + 1), A("z1"), A("yb"), MIN)
-        if first:
-            unit(1)
+        cr = A("crf") if last else A("crow")
 
         def own():
             for b, k in ((0, 2), (1, 3), (2, 6), (3, 7)):
@@ -317,146 +339,117 @@ def rank_program(g, core, T, topo):
             for b in range(2):
                 act(A("fo", C * b, C * b + C), bank(2 + b))
 
-        if not first:
+        def class_row():
+            act(cr, IND(A("rk"), A("k16", 0, 14)))
+
+        def class_hold():
+            hold(A("dc"), cr, A("cd", 0, C))
+
+        for a, e, k in ((0, 128, 0), (128, C, 4)):
+            mm(bank(k, 0, 128), A("qab", 0, 128), A("sab", 0, 128), *half(t, a))
+            mm(bank(k + 1, 0, 128), A("qab", 128, 256), A("sab", 128, 256), *half(t, a))
+            act(A("ya", a, e), bank(k, 0, e - a), AF.Sign, scale=col(SGA), bias=col(EPA))
+            act(A("yb", a, e), bank(k + 1, 0, e - a), AF.Sign, scale=col(SGB), bias=col(EPB))
+            if first:
+                step_row(a // 128, cp)
+            tt(A("xr", a + 1, e + 1), A("ya", a, e), A("yb", a, e), MIN)
+        if first:
+            step_row(2, act)
+            step_row(3, act)
+        else:
             own()
         for s in range(4):
-            scan(A("so1", W * s, W * s + N1), A("cb", W * s, W * s + N1), A("xv", 0, N1), A("in1", s, s + 1))
+            scan(A("so1", W * s, W * s + N1), A("cb", W * s, W * s + N1), A("xr", 0, N1), A("in1", s, s + 1))
+        scan(A("xv", 1, C + 1), A("place"), A("xr", 1, C + 1), -1.0, MAX, MIN)
+        if first:
+            unit(0)
+        else:
+            key_a()
         fin1 = A("so1", N1 - 1, 4 * W, W)
         f16 = A("lst", l0, l0 + 4)
-
-        def behind(s):
-            ts(A("d2", W * s + 1, W * s + 1 + C), A("xv", 1, C + 1), A("so1", W * s + N1 - 1, W * s + N1), ADD, 126.5 / 1024, GT)
-
-        behind(0)
-        behind(1)
-        ts(f16, fin1, -1024.0, MUL, 126.0, ADD)
-        ts(A("in2"), fin1, 2.0, MUL, 160.0 / 512, ADD)
-        behind(2)
-        behind(3)
+        ts(f16, fin1, -512.0, MUL, 159.0, ADD)
+        ts(A("in2"), fin1, 127.0 * D, ADD)
         act(A("frv"), IND(A("tv"), f16))
         for s in range(4):
-            act(A("junk", 64 * s, 64 * s + 64), A("frv"), AF.Sign, acc=A("acc", s, s + 1), scale=1.0 / 1024,
-                bias=A("so1", W * s + N1 - 1, W * s + N1))
+            one = A("so1", W * s + N1 - 1, W * s + N1)
+            ts(A("d2", W * s, W * s + N1 - 1), A("xv", 0, N1 - 1), one, ADD, 159.5 * D, GT)
+            act(A("junk", 64 * s, 64 * s + 64), A("frv"), AF.Sign, acc=A("acc", s, s + 1), scale=D, bias=one)
         for s in range(4):
             scan(A("so2", W * s, W * s + N2), A("cb", W * s, W * s + N2), A("d2", W * s, W * s + N2), A("in2", s, s + 1))
         if first:
-            ts(A("io"), A("tv", 0, 64), 126.0, ADD)
-            unit(2)
+            unit(1)
         else:
-            hold(A("da"), A("ya"), A("cda", 0, C))
+            key_steps_b()
         ts(A("lst", l0 + 4, l0 + 8), A("so2", N2 - 1, 4 * W, W), -512.0, MUL, 255.0, ADD)
         send(to, A("ll", l0, l0 + 8), A("lst", l0, l0 + 8), "larr%d" % t)
-        ts(A("r16"), A("acc"), 0.5, MUL, 31.5, ADD) if False else ts(A("r16"), A("acc"), -0.5, MUL, 31.5, ADD)
-
-        def key_b():
-            ts(A("cdb", 15, C, 16), A("da", 15, C, 16), col(B0), MUL, col(B1), ADD)
-
-        def key_list():
-            ts(A("k16", 0, 14), A("db", 15, C, 16), col(K0), MUL, col(K1), ADD)
-
+        ts(A("r16"), A("acc"), -0.5, MUL, 31.5, ADD)
         if first:
-            unit(3)
+            unit(2)
         else:
             key_b()
         cp(IND(A("srt"), A("r16")), A("io"))
         if first:
-            ts(col(A0), col(SGA), -4.0, MUL)
-            ts(col(A1), col(SGA), -256.0, MUL, end, ADD)
-            ts(col(B0), col(SGA), 2.0, MUL, col(SGB), MUL)
+            unit(3)
         else:
-            hold(A("db"), A("yb"), A("cdb", 0, C))
+            key_list()
         hold(A("sol"), A("srt"), A("cd", 0, 64))
         if first:
-            cp(A("cda"), A("cd"))
-            cp(A("cdb"), A("cd"))
-        else:
-            cp(A("r4"), IND(A("m4"), A("r16"))) if not last else None
+            for b in range(4):
+                fill(A("fh", FW * b + 2 * C, FW * b + FW), 0.0)
+        elif not last:
+            low_keys()
         ts(A("lst", l0 + 8, l0 + 12), A("sol", 15, 64, 16), 64.0, ADD)
         send(to, A("ll", l0 + 8, l0 + 12), A("lst", l0 + 8, l0 + 12), "karr%d" % t)
-        if not first:
-            key_list()
+        if first:
+            lin(col(A0), col(SGA), -4.0, 0.0)
+            lin(col(A1), col(SGA), -256.0, end)
+            lin(col(B0), col(SGA), col(SGB), 0.0)
+            lin(col(K0), col(SGB), -0.5, 0.0)
+            lin(col(K1), col(SGB), -64.0, 1.5)
+            lin(col(B2), end, 1.0, -64.0)
+            lin(col(B1), col(B0), 128.0, col(B2))
+            lin(col(B0), col(B0), 2.0, 0.0)
+            fill(A("zt", 256, 512), 0.0)
+            key_steps()
         lq, ls = A("lq", C * t, C * t + C), A("ls", C * t, C * t + C)
         arrive(frm, 2, "qarr%d" % t, [lq, ls])
         fb = (4, 5, 0, 1)
         for b in range(4):
             unpack(fb[b], b, lq, ls)
-        if first:
-            own()
-
-        def half_s(b, a):
-            act(A("fh", FW * b + a, FW * b + a + C), bank(fb[b]), AF.Identity, scale=0.5)
-
-        def half_v(b):
-            ts(A("fh", FW * b, FW * b + C), bank(fb[b]), 0.5, MUL)
-
-        def again(b):
+        for b in range(4):
+            act(A("fh", FW * b, FW * b + C), bank(fb[b]), AF.Identity, scale=0.5)
+        for b in range(4):
             cp(A("fh", FW * b + C, FW * b + 2 * C), A("fh", FW * b, FW * b + C))
-
-        if first:
-            ops.extend([ops.pop(-2), ops.pop(-1)][::1]) if False else None
-        half_s(0, 0)
-        half_s(2, 0)
-        half_s(2, C)
-        if first:
-            key_steps()
-            ts(col(B1), col(B0), 64.0, MUL, end, ADD)
-        half_v(1)
-        again(0)
-        half_v(3)
-        again(1)
-        if first:
-            hold(A("da"), A("ya"), A("cda", 0, C))
-        again(3)
-        act(A("rk"), IND(A("io"), A("r16")))
         arrive(frm, 1, "larr%d" % t, [A("ll", l0, l0 + 8)])
         arrive(frm, 1, "karr%d" % t, [A("ll", l0 + 8, l0 + 12)])
         if first:
-            ts(col(B1), col(B1), -64.0, ADD)
-            ts(col(K0), col(SGB), -0.5, MUL)
-            ts(col(K1), col(SGB), -64.0, MUL, 1.5, ADD)
-            act(A("zt", 256, 512), A("zero", 0, 256))
-        sec = [IND(A("fh", FW * b, FW * b + FW), A("ll", l0 + 4, l0 + 8)) for b in range(4)]
-        cp(A("zs", 0, 64), sec[0])
-        for b in range(1, 4):
-            act(A("zs", 64 * b, 64 * b + 64), sec[b])
+            key_a()
+            cp(A("cdb"), A("cd"))
+        for b in range(4):
+            act(A("zs", 64 * b, 64 * b + 64), IND(A("fh", FW * b, FW * b + FW), A("ll", l0 + 4, l0 + 8)))
         for b in range(4):
             tt(A("zk", 64 * b, 64 * b + 64), IND(A("fh", FW * b + C, FW * b + FW), A("ll", l0, l0 + 4)), A("zs", 64 * b, 64 * b + 64), ADD)
         for b in range(4):
             (act if b < 2 else cp)(A("zt", b, 256, 4), IND(A("zk", 64 * b, 64 * b + 64), A("ll", l0 + 8, l0 + 12)))
+        act(A("rk"), IND(A("io"), A("r16")))
         quant(A("qz"), A("sz"), A("zt"))
         for b in range(4):
             mm(bank(b, 0, 128), A("wq", 128 * b, 128 * b + 128), A("wsc", 128 * b, 128 * b + 128), A("qz"), A("sz"))
-        cr = A("crf") if last else A("crow")
-
-        def class_row():
-            act(cr, IND(A("rk"), A("k16", 0, 14)))
-
-        def low_rows():
-            cp(A("cm4"), IND(A("r4"), A("k16", 0, 14)))
-
-        def class_hold():
-            hold(A("dc"), cr, A("cd", 0, C))
-
-        def own_part():
-            ts(A("cm16"), A("cm4"), 4.0, MUL)
-
-        def class_list():
-            ts(A("c16", 0, 14), A("dc", 15, C, 16), 64.0, ADD)
-
         if first:
             act(A("ht", 256, 512), A("zero", 0, 256))
+            key_steps_b()
+            low_keys()
             key_b()
-            cp(A("r4"), IND(A("m4"), A("r16")))
-            hold(A("db"), A("yb"), A("cdb", 0, C))
             quant(A("hq", 0, 128), A("hs", 0, 128), A("zero"))
             key_list()
+            fill(A("tn", 4 * C, 4 * P), 0.0)
         else:
             class_row()
             if last:
                 quant(A("qv"), A("sv"), A("vt"))
                 class_hold()
             else:
-                low_rows()
+                low_row()
                 class_hold()
                 own_part()
             class_list()
@@ -468,7 +461,8 @@ def rank_program(g, core, T, topo):
         send(frm, A("hs", h1, h1 + K), A("sh", h0, h0 + K), "harr%d" % t)
         if first:
             class_row()
-            low_rows()
+            own()
+            low_row()
             class_hold()
             own_part()
             class_list()
@@ -477,26 +471,30 @@ def rank_program(g, core, T, topo):
             high_hold()
             high_steps()
             key_steps()
-            pair_hold()
-            pair_list()
         arrive(to, 2, "harr%d" % t, [A("hq", h1, h1 + K), A("hs", h1, h1 + K)])
-        hb_ = (4, 5, 2, 3)
-        for b in (2, 0, 3, 1):
-            unpack(hb_[b], b, A("hq", h1 - K, h1 + K), A("hs", h1 - K, h1 + K), 128)
-        for b in (2, 0, 3, 1):
-            (cp if b < 2 else act)(A("gd", 64 * b, 64 * b + 64), bank(hb_[b], 64, 128))
+        gb = (4, 5, 2, 3)
+        for b in (0, 2, 1, 3):
+            unpack(gb[b], b, A("hq", h1 - K, h1 + K), A("hs", h1 - K, h1 + K), 128)
+        for b in (0, 2, 1, 3):
+            (act if b else cp)(A("gd", 64 * b, 64 * b + 64), bank(gb[b], 64, 128))
         if first:
             dma("Y", "v", lambda: T["vt"][:], lambda: T.v[:], [A("vt")], [A("gd", 0, 64)])
         if last:
             dma("Y", "ol", lambda: T.ol[:], lambda: T["crf"][0:128:16, :], [], [cr, A("c16", 0, 14)])
-        cl = A("c16", 0, 14)
+
+        def by_class(b, a, e):
+            return IND(A("gd", 64 * b, 64 * b + 64), A("c16", a // 16, e // 16))
+
+        parts = ((2, 0, C), (3, 0, 128), (3, 128, C))
+        for b, a, e in parts:
+            act(A("ge", C * (b - 2) + a, C * (b - 2) + e), by_class(b, a, e))
         for b in range(2):
-            tt(A("tn", b, 896, 4), IND(A("gd", 64 * b, 64 * b + 64), cl), A("fo", C * b, C * b + C), ADD)
-        for b in range(2, 4):
-            act(A("ge", C * (b - 2), C * (b - 1)), IND(A("gd", 64 * b, 64 * b + 64), cl))
-        for b in range(2, 4):
-            tt(A("tn", b, 896, 4), A("ge", C * (b - 2), C * (b - 1)), bank(4 + b), ADD)
-        quant(A("qt", C * t + C, C * t + 2 * C), A("st", C * t + C, C * t + 2 * C), A("tn"))
+            if not last:
+                (pair_hold, pair_list)[b]()
+            tt(A("tn", b, 4 * C, 4), by_class(b, 0, C), A("fo", C * b, C * b + C), ADD)
+        for b, a, e in parts:
+            tt(A("tn", 4 * a + b, 4 * e, 4), A("ge", C * (b - 2) + a, C * (b - 2) + e), bank(4 + b, a, e), ADD)
+        state(t + 1, "tn")
         if not last:
             send_state(t + 1)
             step_row(2, act)
@@ -504,11 +502,11 @@ def rank_program(g, core, T, topo):
             step_row(0, cp)
             step_row(1, cp)
 
-    q0 = R * C
-    mm(bank(0, 0, 128), A("qv"), A("sv"), A("qt", q0, q0 + 128), A("st", q0, q0 + 128))
-    mm(bank(1, 0, 128), A("qv"), A("sv"), A("qt", q0 + 96, q0 + C), A("st", q0 + 96, q0 + C))
-    cp(A("yo", 0, 128), bank(0, 0, 128))
-    act(A("yo", 128, C), bank(1, 32, 128))
+    q0 = R * P
+    mm(bank(0, 0, 128), A("qv"), A("sv"), *half(R, 0))
+    mm(bank(1, 0, 128), A("qv"), A("sv"), *half(R, 128))
+    act(A("yo", 0, 128), bank(0, 0, 128))
+    cp(A("yo", 128, C), bank(1, 0, C - 128))
     dma("Y", "oc", lambda: T.oc[:], lambda: T["qt"][:, q0:q0 + C].bitcast(dt.uint8), [], [A("qt", q0, q0 + C)])
     dma("S", "y", lambda: T.y[:], lambda: T["yo"][:], [], [A("yo")])
     for k in range(4):
@@ -522,7 +520,8 @@ def rank_program(g, core, T, topo):
         for name, m in o["wr"]:
             deps |= {j for j, mj, w in seen.get(name, []) if (m & mj).any()}
         for name, m in o["rd"]:
-            deps |= {j for j, mj, w in seen.get(name, []) if w and (m & mj).any()}
+            deps |= {j for j, mj, w in seen.get(name, [])
+                     if (w or name == "ps" and ops[j]["q"] != o["q"]) and (m & mj).any()}
         for name, m in o["wr"]:
             seen.setdefault(name, []).append((i, m, True))
         for name, m in o["rd"]:

import numpy as np
from concourse.bass import DstId, RemoteDMATransfer
from concourse.mybir import dt, AluOpType, ActivationFunctionType

C, K, R = 224, 64, 3
STEP = [1, 2, 4]
P = 256
W = 244
N1, N2 = 227, 228
FW = 512
D = 1.0 / 512
L = 1.0 - D
BF, F32, I32, U16, U8, MX = "bfloat16", "float32", "int32", "uint16", "uint8", "float8_e4m3fn_x4"


def _sb(n, t):
    return ("sbuf", [128, n], t)


SCRATCH = {
    "xt": _sb(4 * P, BF), "ut": _sb(512, BF), "vt": _sb(512, BF), "nx32": _sb(16, I32), "co32": _sb(16, I32),
    "wq": _sb(512, MX), "wsc": _sb(512, U8),
    "qu": _sb(128, MX), "su": _sb(128, U8), "qab": _sb(256, MX), "sab": _sb(256, U8),
    "qv": _sb(128, MX), "sv": _sb(128, U8), "qe": _sb(512, MX), "se": _sb(512, U8),
    "qt": _sb(4 * P, MX), "st": _sb(4 * P, U8), "lq": _sb(3 * C, MX), "ls": _sb(3 * C, U8),
    "qz": _sb(128, MX), "sz": _sb(128, U8), "qh": _sb(3 * 128, MX), "sh": _sb(3 * 128, U8),
    "hq": _sb(128 + 3 * K, MX), "hs": _sb(128 + 3 * K, U8),
    "tn": _sb(4 * P, BF), "zt": _sb(512, BF), "ht": _sb(512, BF), "zero": _sb(512, BF), "eb": _sb(520, BF), "ones": _sb(128, BF),
    "fh": _sb(4 * FW, BF), "fo": _sb(448, BF), "gd": _sb(256, BF), "zs": _sb(256, BF), "zk": _sb(256, BF), "ge": _sb(448, BF),
    "yo": _sb(C, F32),
    "lst": _sb(3 * 16, U16), "ll": _sb(3 * 16, U16), "nx16": _sb(16, U16), "co16": _sb(16, U16), "c16": _sb(16, U16),
    "k16": _sb(16, U16), "p16": _sb(16, U16), "r16": _sb(4, U16), "u16": _sb(16, U16), "cd16": _sb(16, U16), "ct16": _sb(72, U16),
    "ya": _sb(C, BF), "yb": _sb(C, BF), "xr": _sb(W, BF), "xv": _sb(W, BF), "cb": _sb(4 * W, BF), "so1": _sb(4 * W, BF),
    "d2": _sb(4 * W, BF), "so2": _sb(4 * W, BF), "in1": _sb(4, F32), "in2": _sb(4, F32),
    "frv": _sb(64, BF), "junk": _sb(256, BF), "acc": _sb(4, F32), "srt": _sb(64, BF), "sol": _sb(64, BF),
    "da": _sb(C, BF), "db": _sb(C, BF), "rk": _sb(64, BF), "r4": _sb(64, BF), "crow": _sb(C, BF), "crf": _sb(C, F32), "dc": _sb(C, BF),
    "cm4": _sb(C, BF), "cm16": _sb(C, BF), "hb": _sb(W, BF), "dh": _sb(240, BF), "dp": _sb(240, BF),
    "cdp": _sb(240, BF), "cda": _sb(240, BF), "cdb": _sb(240, BF),
    "pi": _sb(1, I32), "ci": _sb(4, I32), "cf": _sb(4, F32), "col": _sb(16, F32), "kt": _sb(4, F32), "u32": _sb(16, I32),
    "c4": _sb(4, F32), "w1": _sb(72, F32), "w3": _sb(72, F32), "w5": _sb(4, F32), "w6": _sb(4, F32),
    "a36": _sb(36, F32), "b36": _sb(36, F32), "n36": _sb(72, F32), "t36": _sb(36, BF), "ctab": _sb(1152, BF),
    "e0": _sb(16, F32), "e1": _sb(16, F32), "wr": _sb(16, F32), "cds": _sb(16, BF), "cd": _sb(240, BF),
    "m4": _sb(64, BF), "io": _sb(64, BF), "tv": _sb(288, BF), "place": _sb(C, BF),
    "ps": ("psum", [128, 4096], F32),
}
LOADS = ["co", "nx", "x", "u", "wc", "ws", "v"]
STORES = ["ol", "oc", "os0", "os1", "os2", "os3", "y"]
SEMAPHORES = (["cV", "cS", "cP", "cG", "sent"] + ["d_" + n for n in LOADS + STORES]
              + [a + str(t) for a in ("qarr", "larr", "karr", "harr") for t in range(R)])
ADD, SUB, MUL, MAX, MIN = AluOpType.add, AluOpType.subtract, AluOpType.mult, AluOpType.max, AluOpType.min
GT, EQ, NE = AluOpType.is_gt, AluOpType.is_equal, AluOpType.not_equal
AND, SHR = AluOpType.bitwise_and, AluOpType.logical_shift_right
AF = ActivationFunctionType


def A(name, a=0, b=None, step=1, cast=None):
    return ("ap", name, a, SCRATCH[name][1][1] if b is None else b, step, cast)


def IND(win, off):
    return ("ind", win, off)


def bank(k, a=0, b=None):
    return A("ps", 512 * k + a, 512 * k + (C if b is None else b))


def _cells(v):
    if v[0] == "ind":
        return _cells(v[1]) + _cells(v[2])
    m = np.zeros(SCRATCH[v[1]][1][1], bool)
    if v[1] == "ps":
        m[v[2] // 512 * 512:v[2] // 512 * 512 + 512] = True
    else:
        m[v[2]:v[3]:v[4]] = True
    return [(v[1], m)]


def rank_program(g, core, T, topo):
    rank = T.rank_of(core)
    if rank is None:
        return
    n = len(T.cores)
    ops = []

    def real(v):
        if not isinstance(v, tuple):
            return v
        if v[0] == "ind":
            return real(v[1]).indirect(real(v[2]))
        r = T[v[1]][:, v[2]:v[3]] if v[4] == 1 else T[v[1]][:, v[2]:v[3]:v[4]]
        return r if v[5] is None else r.bitcast(v[5])

    def op(q, call, outs, ins, sem=None, val=0):
        wr, rd = [], []
        for v in outs:
            if v[0] == "ind":
                wr += _cells(v[1])
                rd += _cells(v[2])
            else:
                wr += _cells(v)
        for v in ins:
            if isinstance(v, tuple):
                rd += _cells(v)
        ops.append({"q": q, "call": call, "wr": wr, "rd": rd, "sem": sem, "val": val})

    def ts(out, a, s1, op0, s2=None, op1=None):
        if op1 is None:
            op("V", lambda: g.vector.tensor_scalar(real(out), real(a), real(s1), None, op0), [out], [a, s1])
        else:
            op("V", lambda: g.vector.tensor_scalar(real(out), real(a), real(s1), real(s2), op0, op1), [out], [a, s1, s2])

    def tt(out, a, b, o):
        op("V", lambda: g.vector.tensor_tensor(real(out), real(a), real(b), o), [out], [a, b])

    def cp(out, a):
        op("V", lambda: g.vector.tensor_copy(real(out), real(a)), [out], [a])

    def fill(out, c):
        op("V", lambda: g.vector.memset(real(out), c), [out], [])

    def scan(out, d0, d1, ini, op0=ADD, op1=MAX):
        op("V", lambda: g.vector.tensor_tensor_scan(real(out), real(d0), real(d1), real(ini), op0, op1), [out], [d0, d1, ini])

    def hold(out, row, steps):
        scan(out, row, steps, -2.0, MAX, ADD)

    def quant(q, s, a):
        op("V", lambda: g.vector.quantize_mx(real(q), real(s), real(a)), [q, s], [a])

    def act(out, a, f=AF.Copy, acc=None, **kw):
        def call():
            k = {x: real(y) for x, y in kw.items()}
            if acc is not None:
                k["accum_out"] = real(acc)
            return g.scalar.activation(real(out), real(a), f, **k)
        op("S", call, [out] + ([] if acc is None else [acc]), [a] + list(kw.values()))

    def lin(out, a, scale, bias):
        act(out, a, AF.Identity, scale=scale, bias=bias)

    def sfill(out, c):
        lin(out, A("zero", 0, len(range(out[2], out[3], out[4]))), 1.0, c)

    def mm(out, wq, wsc, q, s):
        op("P", lambda: g.tensor.matmul_mx(real(out), real(wq), real(wsc), real(q), real(s), True, True), [out], [wq, wsc, q, s])

    def unpack(k, b, q, s, cols=C):
        mm(bank(k, 0, cols), A("qe", 128 * b, 128 * b + 128), A("se", 128 * b, 128 * b + 128), q, s)

    def iota(out, pat, base=0, cm=0):
        if SCRATCH[out[1]][2] == I32:
            op("G", lambda: g.iota(real(out), pat, base, cm), [out], [])
        else:
            op("G", lambda: g.iota(real(out), pat, base, cm, allow_small_or_imprecise_dtypes=True), [out], [])

    def dma(q, name, dst, src, outs, ins):
        e = g.sync if q == "Y" else g.scalar
        op(q, lambda: e.dma_start(dst(), src()), outs, ins, sem="d_" + name, val=16)

    sent = [0]

    def send(to, dst, src, sem):
        rid, pid = topo.addr(to, core)
        sent[0] += len(topo.engines(core, to))
        op("G", lambda: g.remote_dma(real(dst), real(src), T.sem[sem], T.sem["sent"], pid, rid, topo.mask(core, to)),
           [], [src], sem="none")

    def arrive(frm, calls, sem, outs):
        op("X", None, outs, [], sem=sem, val=calls * len(topo.engines(frm, core)))

    def u8(name, a, b):
        return A(name, a, b, 1, dt.uint8)

    def u32(name, a, b):
        return A(name, a, b, 1, dt.uint32)

    def col(k):
        return A("col", k, k + 1)

    SGA, SGB, EPA, EPB, TMP, PC, A0, A1, B0, B1, B2, K0, K1 = range(13)
    icol, qcol, lacol, lbcol = [A("cf", k, k + 1) for k in range(4)]
    end = A("cds", 15, 16)

    def half(t, a):
        return A("qt", P * t + a, P * t + a + 128), A("st", P * t + a, P * t + a + 128)

    def state(t, tile):
        for a in (0, 128):
            quant(*half(t, a), A(tile, 4 * a, 4 * a + 512))

    def send_state(t):
        to = T.cores[(rank + STEP[t]) % n]
        send(to, u8("lq", C * t, C * t + C), u8("qt", P * t, P * t + C), "qarr%d" % t)
        send(to, A("ls", C * t, C * t + C), A("st", P * t, P * t + C), "qarr%d" % t)

    def step_row(s, on):
        on(A("cb", W * s + 1, W * s + 241), IND(A("ctab", 288 * s, 288 * s + 288), A("p16", 0, 15)))

    def own_part():
        ts(A("cm16"), A("cm4"), 4.0, MUL)

    def high_row():
        tt(A("hb", 1, C + 1), IND(A("cm4"), A("nx16", 0, 14)), A("cm16"), ADD)

    def high_hold():
        hold(A("dh"), A("hb", 1, 241), A("cd"))

    def high_steps():
        ts(A("cdp", 15, 240, 16), A("dh", 15, 240, 16), 16.0, MUL, col(PC), ADD)

    def pair_hold():
        hold(A("dp"), A("hb", 0, 240), A("cdp"))

    def pair_list():
        ts(A("p16", 0, 15), A("dp", 15, 240, 16), 256.0, ADD)

    def key_steps():
        ts(A("cda", 15, C, 16), A("dh", 15, C, 16), col(A0), MUL, col(A1), ADD)

    def key_a():
        hold(A("da"), A("ya"), A("cda", 0, C))

    def key_steps_b():
        ts(A("cdb", 15, C, 16), A("da", 15, C, 16), col(B0), MUL, col(B1), ADD)

    def key_b():
        hold(A("db"), A("yb"), A("cdb", 0, C))

    def key_list():
        ts(A("k16", 0, 14), A("db", 15, C, 16), col(K0), MUL, col(K1), ADD)

    def low_keys():
        cp(A("r4"), IND(A("m4"), A("r16")))

    def low_row():
        cp(A("cm4"), IND(A("r4"), A("k16", 0, 14)))

    def class_list():
        ts(A("c16", 0, 14), A("dc", 15, C, 16), 64.0, ADD)

    def unit(b):
        quant(A("qe", 128 * b, 128 * b + 128), A("se", 128 * b, 128 * b + 128), A("eb", 3 - b, 515 - b))

    dma("Y", "co", lambda: T["co32"][:, 0:14], lambda: T.co[:], [A("co32", 0, 14)], [])
    dma("S", "x", lambda: T["xt"][:, 0:4 * C], lambda: T.x[:], [A("xt", 0, 4 * C)], [])
    dma("Y", "nx", lambda: T["nx32"][:, 0:14], lambda: T.nx[:], [A("nx32", 0, 14)], [])
    dma("Y", "u", lambda: T["ut"][:], lambda: T.u[:], [A("ut")], [])
    dma("Y", "wc", lambda: T["wq"][:].bitcast(dt.uint8), lambda: T.wc[:], [A("wq")], [A("ut")])
    dma("Y", "ws", lambda: T["wsc"][:], lambda: T.ws[:], [A("wsc")], [])

    iota(A("pi"), [[1, 1]], 0, 1)
    iota(A("c4"), [[-4, 4]])
    iota(A("a36"), [[1, 6], [0, 6]], -1)
    iota(A("b36"), [[0, 6], [1, 6]], -1)
    iota(A("w1"), [[-4, 4], [1, 18]])
    iota(A("io"), [[1, 64]])
    iota(A("m4"), [[0, 16], [1, 4]])
    iota(A("u32"), [[1, 2], [16, 8]])
    iota(A("tv"), [[1, 288]], -159)
    fill(A("zero"), 0.0)
    fill(A("hb"), 0.0)
    ts(A("ci", 0, 1), A("pi"), 15, AND)
    ts(A("ci", 1, 2), A("pi"), 2, SHR, 3, AND)
    ts(A("ci", 2, 3), A("pi"), 1, SHR, 1, AND)
    ts(A("ci", 3, 4), A("pi"), 1, AND)
    fill(A("eb"), 0.0)
    cp(A("cf"), A("ci"))
    fill(A("xr"), -1.0)
    fill(A("e0", 15, 16), -128.0)
    sfill(A("xt", 4 * C, 4 * P), 0.0)
    sfill(A("hb", 225, 227), 16.0)
    sfill(A("hb", 227, 228), 16.25)
    sfill(A("ones"), 1.0)
    sfill(A("xv", 0, W, C + 1), -1.0)
    sfill(A("d2", N2 - 1, 4 * W, W), -2.0)
    sfill(A("d2", N2 - 2, 4 * W, W), -2.0)
    ts(A("w5"), A("c4"), icol, ADD, -1.0, MAX)
    ts(A("n36", 0, 36), A("a36"), qcol, NE, D, MAX)
    ts(A("n36", 36, 72), A("b36"), qcol, NE, L, MUL)
    ts(A("w3"), A("w1"), -1.0, MAX, 4.0, MIN)
    ts(A("w6"), A("w5"), 4.0, MIN, 7.0, ADD)
    ts(A("wr"), A("io", 0, 16), icol, SUB)
    tt(A("t36"), A("n36", 0, 36), A("n36", 36, 72), SUB)
    ts(A("cd16"), A("io", 0, 16), 0.0, MUL, icol, ADD)
    for s in range(4):
        ts(A("ct16", 18 * s, 18 * s + 18), A("w3", 18 * s, 18 * s + 18), 6.0, MUL, A("w6", s, s + 1), ADD)
    ts(A("e0", 0, 15), A("wr", 0, 15), -1.0, EQ, -256.0, MUL)
    ts(A("e1"), A("wr"), 0.0, EQ, 64.0, MUL)
    lin(col(SGA), lacol, -2.0, 1.0)
    lin(col(SGB), lbcol, -2.0, 1.0)
    lin(col(TMP), icol, -D, 286.0 * D)
    lin(col(EPA), col(SGA), 2.0 ** -120, 0.0)
    lin(col(EPB), col(SGB), 2.0 ** -120, 0.0)
    lin(A("kt"), A("m4", 0, 4), 4.0, qcol)
    lin(A("in1"), A("m4", 0, 4), -16.0 * D, col(TMP))
    act(A("ctab", 0, 576), IND(A("t36"), A("ct16", 0, 36)))
    act(A("ctab", 576, 1152), IND(A("t36"), A("ct16", 36, 72)))

    cp(A("co16", 0, 14), A("co32", 0, 14))
    cp(A("nx16", 0, 14), A("nx32", 0, 14))
    tt(A("cds"), A("e0"), A("e1"), ADD)
    cp(A("u16"), A("u32"))
    cp(A("cm4"), IND(A("m4"), A("co16", 0, 14)))
    cp(A("cd"), IND(A("cds"), A("cd16", 0, 15)))
    own_part()
    state(0, "xt")
    send_state(0)
    op("G", lambda: g.affine_select(T["eb"][:, 3:515:4], T["ones"][:], [[1, 128]], EQ, 0.0, 0, -1), [A("eb", 3, 515, 4)], [A("ones")])
    high_row()
    quant(A("qu"), A("su"), A("ut"))
    lin(col(PC), end, 1.0, 832.0)
    cp(A("cdp"), A("cd"))
    high_hold()
    act(A("sab", 0, 128), IND(A("su"), A("u16", 0, 8)))
    act(A("sab", 128, 256), IND(A("su"), A("u16", 8, 16)))
    sfill(A("ctab", 272, 1152, 288), -2.125)
    sfill(A("ctab", 276, 1152, 288), 0.1875)
    lin(A("place"), A("tv", 0, C), D, 159.0 * D)
    cp(u32("qab", 0, 128), IND(u32("qu", 0, 128), A("u16", 0, 8)))
    high_steps()
    cp(u32("qab", 128, 256), IND(u32("qu", 0, 128), A("u16", 8, 16)))
    pair_hold()
    ts(A("cb", 0, 4 * W, W), A("kt"), 0.0, NE, D, MAX)
    cp(A("cda"), A("cd"))
    pair_list()

    for t in range(R):
        first, last = t == 0, t == R - 1
        to = T.cores[(rank + STEP[t]) % n]
        frm = T.cores[(rank - STEP[t]) % n]
        qt, st = A("qt", P * t, P * t + C), A("st", P * t, P * t + C)
        l0 = 16 * t
        cr = A("crf") if last else A("crow")

        def own():
            for b, k in ((0, 2), (1, 3), (2, 6), (3, 7)):
                unpack(k, b, qt, st)
            for b in range(2):
                act(A("fo", C * b, C * b + C), bank(2 + b))

        def class_row():
            act(cr, IND(A("rk"), A("k16", 0, 14)))

        def class_hold():
            hold(A("dc"), cr, A("cd", 0, C))

        for a, e, k in ((0, 128, 0), (128, C, 4)):
            mm(bank(k, 0, 128), A("qab", 0, 128), A("sab", 0, 128), *half(t, a))
            mm(bank(k + 1, 0, 128), A("qab", 128, 256), A("sab", 128, 256), *half(t, a))
            act(A("ya", a, e), bank(k, 0, e - a), AF.Sign, scale=col(SGA), bias=col(EPA))
            act(A("yb", a, e), bank(k + 1, 0, e - a), AF.Sign, scale=col(SGB), bias=col(EPB))
            if first:
                step_row(a // 128, cp)
            tt(A("xr", a + 1, e + 1), A("ya", a, e), A("yb", a, e), MIN)
        if first:
            step_row(2, act)
            step_row(3, act)
        else:
            own()
        for s in range(4):
            scan(A("so1", W * s, W * s + N1), A("cb", W * s, W * s + N1), A("xr", 0, N1), A("in1", s, s + 1))
        scan(A("xv", 1, C + 1), A("place"), A("xr", 1, C + 1), -1.0, MAX, MIN)
        if first:
            unit(0)
        else:
            key_a()
        fin1 = A("so1", N1 - 1, 4 * W, W)
        f16 = A("lst", l0, l0 + 4)
        ts(f16, fin1, -512.0, MUL, 159.0, ADD)
        ts(A("in2"), fin1, 127.0 * D, ADD)
        act(A("frv"), IND(A("tv"), f16))
        for s in range(4):
            one = A("so1", W * s + N1 - 1, W * s + N1)
            ts(A("d2", W * s, W * s + N1 - 1), A("xv", 0, N1 - 1), one, ADD, 159.5 * D, GT)
            act(A("junk", 64 * s, 64 * s + 64), A("frv"), AF.Sign, acc=A("acc", s, s + 1), scale=D, bias=one)
        for s in range(4):
            scan(A("so2", W * s, W * s + N2), A("cb", W * s, W * s + N2), A("d2", W * s, W * s + N2), A("in2", s, s + 1))
        if first:
            unit(1)
        else:
            key_steps_b()
        ts(A("lst", l0 + 4, l0 + 8), A("so2", N2 - 1, 4 * W, W), -512.0, MUL, 255.0, ADD)
        send(to, A("ll", l0, l0 + 8), A("lst", l0, l0 + 8), "larr%d" % t)
        ts(A("r16"), A("acc"), -0.5, MUL, 31.5, ADD)
        if first:
            unit(2)
        else:
            key_b()
        cp(IND(A("srt"), A("r16")), A("io"))
        if first:
            unit(3)
        else:
            key_list()
        hold(A("sol"), A("srt"), A("cd", 0, 64))
        if first:
            for b in range(4):
                fill(A("fh", FW * b + 2 * C, FW * b + FW), 0.0)
        elif not last:
            low_keys()
        ts(A("lst", l0 + 8, l0 + 12), A("sol", 15, 64, 16), 64.0, ADD)
        send(to, A("ll", l0 + 8, l0 + 12), A("lst", l0 + 8, l0 + 12), "karr%d" % t)
        if first:
            lin(col(A0), col(SGA), -4.0, 0.0)
            lin(col(A1), col(SGA), -256.0, end)
            lin(col(B0), col(SGA), col(SGB), 0.0)
            lin(col(K0), col(SGB), -0.5, 0.0)
            lin(col(K1), col(SGB), -64.0, 1.5)
            lin(col(B2), end, 1.0, -64.0)
            lin(col(B1), col(B0), 128.0, col(B2))
            lin(col(B0), col(B0), 2.0, 0.0)
            fill(A("zt", 256, 512), 0.0)
            key_steps()
        lq, ls = A("lq", C * t, C * t + C), A("ls", C * t, C * t + C)
        arrive(frm, 2, "qarr%d" % t, [lq, ls])
        fb = (4, 5, 0, 1)
        for b in range(4):
            unpack(fb[b], b, lq, ls)
        for b in range(4):
            act(A("fh", FW * b, FW * b + C), bank(fb[b]), AF.Identity, scale=0.5)
        for b in range(4):
            cp(A("fh", FW * b + C, FW * b + 2 * C), A("fh", FW * b, FW * b + C))
        arrive(frm, 1, "larr%d" % t, [A("ll", l0, l0 + 8)])
        arrive(frm, 1, "karr%d" % t, [A("ll", l0 + 8, l0 + 12)])
        if first:
            key_a()
            cp(A("cdb"), A("cd"))
        for b in range(4):
            act(A("zs", 64 * b, 64 * b + 64), IND(A("fh", FW * b, FW * b + FW), A("ll", l0 + 4, l0 + 8)))
        for b in range(4):
            tt(A("zk", 64 * b, 64 * b + 64), IND(A("fh", FW * b + C, FW * b + FW), A("ll", l0, l0 + 4)), A("zs", 64 * b, 64 * b + 64), ADD)
        for b in range(4):
            (act if b < 2 else cp)(A("zt", b, 256, 4), IND(A("zk", 64 * b, 64 * b + 64), A("ll", l0 + 8, l0 + 12)))
        act(A("rk"), IND(A("io"), A("r16")))
        quant(A("qz"), A("sz"), A("zt"))
        for b in range(4):
            mm(bank(b, 0, 128), A("wq", 128 * b, 128 * b + 128), A("wsc", 128 * b, 128 * b + 128), A("qz"), A("sz"))
        if first:
            act(A("ht", 256, 512), A("zero", 0, 256))
            key_steps_b()
            low_keys()
            key_b()
            quant(A("hq", 0, 128), A("hs", 0, 128), A("zero"))
            key_list()
            fill(A("tn", 4 * C, 4 * P), 0.0)
        else:
            class_row()
            if last:
                quant(A("qv"), A("sv"), A("vt"))
                class_hold()
            else:
                low_row()
                class_hold()
                own_part()
            class_list()
        for b in range(4):
            act(A("ht", b, 256, 4), bank(b, 0, 64), AF.Relu, scale=0.03125)
        h0, h1 = 128 * t, 128 + K * t
        quant(A("qh", h0, h0 + 128), A("sh", h0, h0 + 128), A("ht"))
        send(frm, u8("hq", h1, h1 + K), u8("qh", h0, h0 + K), "harr%d" % t)
        send(frm, A("hs", h1, h1 + K), A("sh", h0, h0 + K), "harr%d" % t)
        if first:
            class_row()
            own()
            low_row()
            class_hold()
            own_part()
            class_list()
        if not last:
            high_row()
            high_hold()
            high_steps()
            key_steps()
        arrive(to, 2, "harr%d" % t, [A("hq", h1, h1 + K), A("hs", h1, h1 + K)])
        gb = (4, 5, 2, 3)
        for b in (0, 2, 1, 3):
            unpack(gb[b], b, A("hq", h1 - K, h1 + K), A("hs", h1 - K, h1 + K), 128)
        for b in (0, 2, 1, 3):
            (act if b else cp)(A("gd", 64 * b, 64 * b + 64), bank(gb[b], 64, 128))
        if first:
            dma("Y", "v", lambda: T["vt"][:], lambda: T.v[:], [A("vt")], [A("gd", 0, 64)])
        if last:
            dma("Y", "ol", lambda: T.ol[:], lambda: T["crf"][0:128:16, :], [], [cr, A("c16", 0, 14)])

        def by_class(b, a, e):
            return IND(A("gd", 64 * b, 64 * b + 64), A("c16", a // 16, e // 16))

        parts = ((2, 0, C), (3, 0, 128), (3, 128, C))
        for b, a, e in parts:
            act(A("ge", C * (b - 2) + a, C * (b - 2) + e), by_class(b, a, e))
        for b in range(2):
            if not last:
                (pair_hold, pair_list)[b]()
            tt(A("tn", b, 4 * C, 4), by_class(b, 0, C), A("fo", C * b, C * b + C), ADD)
        for b, a, e in parts:
            tt(A("tn", 4 * a + b, 4 * e, 4), A("ge", C * (b - 2) + a, C * (b - 2) + e), bank(4 + b, a, e), ADD)
        state(t + 1, "tn")
        if not last:
            send_state(t + 1)
            step_row(2, act)
            step_row(3, act)
            step_row(0, cp)
            step_row(1, cp)

    q0 = R * P
    mm(bank(0, 0, 128), A("qv"), A("sv"), *half(R, 0))
    mm(bank(1, 0, 128), A("qv"), A("sv"), *half(R, 128))
    act(A("yo", 0, 128), bank(0, 0, 128))
    cp(A("yo", 128, C), bank(1, 0, C - 128))
    dma("Y", "oc", lambda: T.oc[:], lambda: T["qt"][:, q0:q0 + C].bitcast(dt.uint8), [], [A("qt", q0, q0 + C)])
    dma("S", "y", lambda: T.y[:], lambda: T["yo"][:], [], [A("yo")])
    for k in range(4):
        dma("Y", "os%d" % k, lambda k=k: T.osc[4 * k:4 * k + 4, :], lambda k=k: T["st"][32 * k:32 * k + 4, q0:q0 + C],
            [], [A("st", q0, q0 + C)])

    seen, known, waited = {}, {q: set() for q in "VSPGY"}, set()
    last_on = {}
    for i, o in enumerate(ops):
        deps = set()
        for name, m in o["wr"]:
            deps |= {j for j, mj, w in seen.get(name, []) if (m & mj).any()}
        for name, m in o["rd"]:
            deps |= {j for j, mj, w in seen.get(name, [])
                     if (w or name == "ps" and ops[j]["q"] != o["q"]) and (m & mj).any()}
        for name, m in o["wr"]:
            seen.setdefault(name, []).append((i, m, True))
        for name, m in o["rd"]:
            seen.setdefault(name, []).append((i, m, False))
        deps.discard(i)
        o["waits"] = []
        if o["q"] == "X":
            o["done"] = {i}
            continue
        kn = known[o["q"]]
        for j in sorted(deps, reverse=True):
            if j not in kn:
                o["waits"].append(j)
                waited.add(j)
                kn |= ops[j]["done"]
        o["done"] = set(kn) | {i}
        if o["sem"] is None:
            o["done"] |= last_on.get(o["q"], set())
            last_on[o["q"]] = o["done"]
    count = {q: 0 for q in "VSPG"}
    for i, o in enumerate(ops):
        if o["sem"] is None and i in waited:
            count[o["q"]] += 1
            o["sem"], o["val"], o["inc"] = "c" + o["q"], count[o["q"]], 1
    queue = {"V": g.vector, "S": g.scalar, "P": g.tensor, "G": g, "Y": g.sync}
    for i, o in enumerate(ops):
        if o["q"] == "X":
            continue
        for j in o["waits"]:
            queue[o["q"]].wait_ge(T.sem[ops[j]["sem"]], ops[j]["val"])
        ins = o["call"]()
        if o["sem"] is not None and o["sem"] != "none":
            ins.then_inc(T.sem[o["sem"]], o.get("inc", 16))
    g.wait_ge(T.sem["sent"], sent[0])
    for name in STORES:
        g.wait_ge(T.sem["d_" + name], 16)
